import numpy as np
import ml_dtypes


def mxq(x, axis, fmt="e4m3"):
    dtype, down = {"e4m3": (ml_dtypes.float8_e4m3fn, 7), "e5m2": (ml_dtypes.float8_e5m2, 14)}[fmt]
    v = np.moveaxis(np.asarray(x, np.float32).astype(ml_dtypes.bfloat16).astype(np.float64), axis, -1)
    blocks = v.reshape(v.shape[:-1] + (-1, 32))
    amax = np.abs(blocks).max(-1, keepdims=True)
    byte = np.maximum(np.where(amax > 0, np.frexp(amax)[1] - 1 + 127, 0) - down, 1)
    scale = np.exp2(byte - 127.0)
    codes = (blocks / scale).astype(np.float32).astype(dtype).astype(np.float64)
    return np.moveaxis((codes * scale).reshape(v.shape), -1, axis)


WIDE = False


def mx_kscale(k):
    if not WIDE:
        return np.ones(k)
    levels = np.array([10, -10, 5, -5, 0])
    if k % 512:
        return np.exp2(np.random.permutation(np.resize(levels, k // 32))).repeat(32)
    a = np.empty((k // 512, 16))
    for p in range(k // 512):
        a[p, :8] = np.random.permutation(np.resize(levels, 8))
        for g in range(8):
            far = levels[np.abs(levels - a[p, g]) >= 10]
            a[p, g + 8] = far[np.random.randint(len(far))]
    return np.exp2(a.ravel()).repeat(32)


def f64(x):
    return np.asarray(x).astype(np.float64)


def striped(idx):
    return np.tile(idx.reshape(-1, 16).T, (8, 1)).astype(np.uint16)


def unstriped(offs):
    return offs[:16].T.reshape(-1).astype(np.int64)


E2M1 = np.array([0.0, 0.5, 1.0, 1.5, 2.0, 3.0, 4.0, 6.0, -0.0, -0.5, -1.0, -1.5, -2.0, -3.0, -4.0, -6.0])


def pack_weight(w, fmt):
    k, n = w.shape
    w = f64(np.asarray(w, np.float32).astype(ml_dtypes.bfloat16)).reshape(k // 32, 32, n)
    amax = np.abs(w).max(1)
    if fmt == "e4m3":
        byte = np.frexp(amax)[1] - 1 + 127 - 7
    else:
        mant, ex = np.frexp(amax / 6.0)
        byte = np.where(mant > 0.5, ex, ex - 1) + 127
    byte = np.clip(np.where(amax > 0, byte, 1), 1, 254)
    scaled = (w * np.exp2(127.0 - byte)[:, None, :]).reshape(k, n).astype(np.float32)
    by_word = np.ascontiguousarray(scaled.reshape(k // 512, 128, 4, n).transpose(0, 1, 3, 2))
    if fmt == "e4m3":
        words = by_word.astype(ml_dtypes.float8_e4m3fn).view(np.uint8)
    else:
        c = by_word.astype(ml_dtypes.float4_e2m1fn).view(np.uint8) & 0xF
        words = (c[..., 0::2] | (c[..., 1::2] << 4)).reshape(k // 512, 128, 2 * n)
    return np.ascontiguousarray(words), np.ascontiguousarray(byte.astype(np.uint8).reshape(k // 512, 16, n))


def unpack_weight(words, scales, fmt):
    g, _, n = scales.shape
    words = np.ascontiguousarray(words).reshape(g, 128, n, -1)
    if fmt == "e4m3":
        vals = words.view(ml_dtypes.float8_e4m3fn).astype(np.float64)
    else:
        nib = np.empty((g, 128, n, 4), np.uint8)
        nib[..., 0::2] = words & 0xF
        nib[..., 1::2] = words >> 4
        vals = E2M1[nib]
    vals = vals * np.repeat(np.exp2(scales.astype(np.float64) - 127.0), 8, axis=1)[..., None]
    return vals.transpose(0, 1, 3, 2).reshape(g * 512, n)


def relu(v):
    return np.maximum(v, 0.0)


K, T, E, G, H, N = 1024, 512, 4, 2, 512, 256


def setup_inputs():
    n = np.random.standard_normal
    s = mx_kscale(K)
    u = mx_kscale(H)
    chosen = np.random.permutation(E)[:G]
    x = pack_weight(n((K, T)) * s[:, None], "e4m3")
    w1 = pack_weight(n((K, E * H)) / np.sqrt(K) / s[:, None] * np.tile(u, E), "e4m3")
    w2 = pack_weight(n((H, E * N)) / np.sqrt(H) / u[:, None], "e4m3")
    return {
        "x_words": x[0],
        "x_scales": x[1],
        "w1_words": w1[0],
        "w1_scales": w1[1],
        "w2_words": w2[0],
        "w2_scales": w2[1],
        "gate": np.stack([np.tile(r, (128, 1)) for r in np.random.uniform(0.2, 1.0, (G, T))]).astype(np.float32),
        "offs": striped((chosen[:, None] * H + np.arange(H)).reshape(-1)),
        "offs2": striped((chosen[:, None] * N + np.arange(N)).reshape(-1)),
    }


def reference(x_words, x_scales, w1_words, w1_scales, w2_words, w2_scales, gate, offs, offs2):
    idx, idx2 = unstriped(offs), unstriped(offs2)
    x = unpack_weight(x_words, x_scales, "e4m3")
    w1 = unpack_weight(w1_words, w1_scales, "e4m3")[:, idx]
    w2 = unpack_weight(w2_words, w2_scales, "e4m3")[:, idx2]
    y = np.zeros((N, T))
    for r in range(G):
        h = f64(gate[r, :1]) * relu(w1[:, r * H:(r + 1) * H].T @ x)
        y = y + w2[:, r * N:(r + 1) * N].T @ mxq(h, 0, "e4m3")
    return y

@@ -1,0 +1,185 @@
+from contextlib import ExitStack
+
+import concourse.mybir as mybir
+
+K, T, E, G, H, N = 1024, 512, 4, 2, 512, 256
+FLOPS = 2 * G * T * (K * H + H * N)
+
+F32 = mybir.dt.float32
+BF16 = mybir.dt.bfloat16
+I32 = mybir.dt.int32
+U32 = mybir.dt.uint32
+U16 = mybir.dt.uint16
+U8 = mybir.dt.uint8
+FP8X4 = mybir.dt.float8_e4m3fn_x4
+MAX = mybir.AluOpType.max
+MULT = mybir.AluOpType.mult
+
+P = 128
+PACK = 4
+PASSES = K // (P * PACK)
+TT = 128
+NT = T // TT
+HALF = T // 2
+X_ROW = 12
+W2_ROW = 8
+WARM = 4
+
+
+def tile_moe_wsel_b_relu_p_kernel(
+    tc, x_words, x_scales, w1_words, w1_scales, w2_words, w2_scales, gate, offs, offs2, out
+):
+    nc = tc.nc
+    with ExitStack() as ctx:
+        keep = ctx.enter_context(tc.tile_pool(name="keep", bufs=1))
+        work = ctx.enter_context(tc.tile_pool(name="work", bufs=3))
+        ps1 = ctx.enter_context(tc.psum_pool(name="ps1", bufs=6))
+        ps2 = ctx.enter_context(tc.psum_pool(name="ps2", bufs=2))
+
+        list1 = keep.tile([P, G * H // 16], U16, name="list1")
+        list2 = keep.tile([P, G * N // 16], U16, name="list2")
+        w1_all = [keep.tile([P, E * H], U32, name="w1_all%d" % s, align_bytes=64) for s in range(PASSES)]
+        w1s_all = keep.tile([P, E * H], U8, name="w1s_all", align_bytes=64)
+        w2_all = keep.tile([P, E * N], U32, name="w2_all", align_bytes=64)
+        w2s_all = keep.tile([P, E * N], U8, name="w2s_all", align_bytes=64)
+        xs = keep.tile([P, PASSES, T], U8, name="xs", align_bytes=64)
+        xw = [keep.tile([P, PASSES, HALF], U32, name="xw%d" % h, align_bytes=64) for h in range(2)]
+        gt = [keep.tile([P, G, HALF], F32, name="gt%d" % h, align_bytes=64) for h in range(2)]
+
+        nc.vector.memset(w1s_all[:].bitcast(I32), 0)
+        nc.gpsimd.memset(w2s_all[:].bitcast(I32), 0)
+        nc.vector.memset(xs[:].bitcast(I32), 0)
+
+        x_hbm = x_words.rearrange("s p t d -> p s (t d)").bitcast(I32)
+        gate_hbm = gate.rearrange("r p t -> p r t")
+
+        nc.sync.dma_start(list1[:], offs)
+        for q in range(4):
+            nc.sync.dma_start(w1s_all[:].bitcast(I32)[32 * q : 32 * q + 8, :], w1_scales.bitcast(I32)[:, 4 * q : 4 * q + 4, :])
+        nc.sync.dma_start(w1_all[0][:].bitcast(I32), w1_words[0].rearrange("p m d -> p (m d)").bitcast(I32))
+        nc.sync.dma_start(list2[:], offs2)
+        nc.sync.dma_start(w1_all[1][:].bitcast(I32), w1_words[1].rearrange("p m d -> p (m d)").bitcast(I32))
+        for q in range(4):
+            r0 = 32 * q + W2_ROW
+            nc.gpsimd.dma_start(w2s_all[:].bitcast(I32)[r0 : r0 + 4, :], w2_scales.bitcast(I32)[0, 4 * q : 4 * q + 4, :])
+        for q in range(4):
+            r0 = 32 * q + X_ROW
+            nc.sync.dma_start(
+                xs[:].bitcast(I32)[r0 : r0 + 4],
+                x_scales.bitcast(I32)[:, 4 * q : 4 * q + 4, :].rearrange("s j t -> j s t"),
+            )
+        nc.sync.dma_start(xw[0][:].bitcast(I32), x_hbm[:, :, 0:HALF])
+        nc.sync.dma_start(gt[0][:], gate_hbm[:, :, 0:HALF])
+        nc.sync.dma_start(xw[1][:].bitcast(I32), x_hbm[:, :, HALF:T])
+        nc.sync.dma_start(w2_all[:].bitcast(I32), w2_words[0].rearrange("p m d -> p (m d)").bitcast(I32))
+        nc.sync.dma_start(gt[1][:], gate_hbm[:, :, HALF:T])
+
+        w1s_sel = keep.tile([P, G * H], U8, name="w1s_sel", align_bytes=64)
+        w1s = keep.tile([P, G, PACK, P], U8, name="w1s", align_bytes=64)
+        w1 = [[keep.tile([P, PACK, P], U32, name="w1_%d_%d" % (s, r), align_bytes=64) for r in range(G)] for s in range(PASSES)]
+        w2 = keep.tile([P, G * N], U32, name="w2", align_bytes=64)
+        w2s = keep.tile([P, G * N], U8, name="w2s", align_bytes=64)
+
+        nc.vector.tensor_copy(w1s_sel[:], w1s_all[:].indirect(list1[:]))
+        nc.vector.tensor_copy(w1s[:].rearrange("p r d m -> p r m d"), w1s_sel[:].rearrange("p (r m d) -> p r m d", r=G, d=PACK))
+
+        def gather_w1(s, r):
+            cols = slice(r * H // 16, (r + 1) * H // 16)
+            nc.vector.tensor_copy(w1[s][r][:].rearrange("p d m -> p m d"), w1_all[s][:].indirect(list1[:, cols]))
+
+        for r in range(G):
+            gather_w1(0, r)
+        nc.vector.tensor_copy(w2s[:], w2s_all[:].indirect(list2[:]))
+
+        warm = ps2.tile([P, 4 * P], F32, name="warm", tag="acc2")
+        for i in range(WARM):
+            nc.tensor.matmul_mx(
+                warm[:],
+                lhsT=w1[0][0][:, 0, :].bitcast(FP8X4),
+                lhsT_scale=w1s[:, 0, 0, :],
+                rhs=w1[0][0][:].rearrange("p d m -> p (d m)").bitcast(FP8X4),
+                rhs_scale=w1s[:, 0].rearrange("p d m -> p (d m)"),
+                start=True,
+                stop=True,
+            )
+
+        for r in range(G):
+            gather_w1(1, r)
+
+        def layer1(j, r):
+            h, c0 = divmod(j * TT, HALF)
+            acc = ps1.tile([P, PACK, TT], F32, name="acc", tag="acc1")
+            for d in range(PACK):
+                for s in range(PASSES):
+                    nc.tensor.matmul_mx(
+                        acc[:, d, :],
+                        lhsT=w1[s][r][:, d, :].bitcast(FP8X4),
+                        lhsT_scale=w1s[4 * s :, r, d, :],
+                        rhs=xw[h][:, s, c0 : c0 + TT].bitcast(FP8X4),
+                        rhs_scale=xs[X_ROW:, s, j * TT : (j + 1) * TT],
+                        start=(s == 0),
+                        stop=(s == PASSES - 1),
+                    )
+            hb = work.tile([P, TT, PACK], BF16, name="hb", align_bytes=64)
+            nc.vector.scalar_tensor_tensor(
+                hb[:],
+                acc[:].rearrange("p d t -> p t d"),
+                0.0,
+                gt[h][:, r, c0 : c0 + TT].unsqueeze(2).to_broadcast([P, TT, PACK]),
+                MAX,
+                MULT,
+            )
+            return hb
+
+        def quantise(hb):
+            hq = work.tile([P, TT], U32, name="hq", align_bytes=64, bufs=4)
+            hs = work.tile([P, TT], U8, name="hs", align_bytes=64, bufs=4)
+            nc.vector.quantize_mx(hq[:].bitcast(FP8X4), hs[:], hb[:].rearrange("p t d -> p (t d)"))
+            return hq, hs
+
+        out_hbm = out.rearrange("(c p) t -> p c t", p=P)
+
+        def pass2(acc, c, r, q):
+            cols = slice(r * N + c * P, r * N + (c + 1) * P)
+            nc.tensor.matmul_mx(
+                acc,
+                lhsT=w2[:, cols].bitcast(FP8X4),
+                lhsT_scale=w2s[W2_ROW:, cols],
+                rhs=q[0][:].bitcast(FP8X4),
+                rhs_scale=q[1][:],
+                start=(r == 0),
+                stop=(r == G - 1),
+            )
+
+        def layer2(j, qs):
+            acc = ps2.tile([P, 2, TT], F32, name="acc2", tag="acc2")
+            for c in range(2):
+                for r in range(G):
+                    pass2(acc[:, c, :], c, r, qs[r])
+            res = work.tile([P, 2, TT], F32, name="res")
+            nc.scalar.copy(res[:], acc[:])
+            nc.sync.dma_start(out_hbm[:, :, j * TT : (j + 1) * TT], res[:])
+
+        def layer2_last(j, qs):
+            accs = [ps1.tile([P, TT], F32, name="acc_last%d" % c, tag="acc1") for c in range(2)]
+            for r in range(G):
+                for c in range(2):
+                    pass2(accs[c][:], c, r, qs[r])
+            res = [keep.tile([P, TT], F32, name="res_last%d" % c) for c in range(2)]
+            nc.scalar.copy(res[0][:], accs[0][:])
+            nc.vector.tensor_copy(res[1][:], accs[1][:])
+            nc.scalar.dma_start(out_hbm[:, 0, j * TT : (j + 1) * TT], res[0][:])
+            nc.sync.dma_start(out_hbm[:, 1, j * TT : (j + 1) * TT], res[1][:])
+
+        units = [(j, r) for j in range(NT) for r in range(G)]
+        hbs, qs = {}, {}
+        for u in range(len(units) + 1):
+            if u < len(units):
+                hbs[u] = layer1(*units[u])
+            if u == 2:
+                nc.vector.tensor_copy(w2[:], w2_all[:].indirect(list2[:]))
+            if u >= 1:
+                qs[u - 1] = quantise(hbs[u - 1])
+            if u >= 2 and u % 2 == 0:
+                j = u // 2 - 1
+                (layer2_last if j == NT - 1 else layer2)(j, [qs[u - 2], qs[u - 1]])

@@ -23,7 +23,7 @@ NT = T // TT
 HALF = T // 2
 X_ROW = 12
 W2_ROW = 8
-WARM = 4
+WARM = 3
 
 
 def tile_moe_wsel_b_relu_p_kernel(
@@ -32,36 +32,46 @@ def tile_moe_wsel_b_relu_p_kernel(
     nc = tc.nc
     with ExitStack() as ctx:
         keep = ctx.enter_context(tc.tile_pool(name="keep", bufs=1))
+        stage = ctx.enter_context(tc.tile_pool(name="stage", bufs=1))
         work = ctx.enter_context(tc.tile_pool(name="work", bufs=3))
         ps1 = ctx.enter_context(tc.psum_pool(name="ps1", bufs=6))
         ps2 = ctx.enter_context(tc.psum_pool(name="ps2", bufs=2))
 
         list1 = keep.tile([P, G * H // 16], U16, name="list1")
         list2 = keep.tile([P, G * N // 16], U16, name="list2")
-        w1_all = [keep.tile([P, E * H], U32, name="w1_all%d" % s, align_bytes=64) for s in range(PASSES)]
         w1s_all = keep.tile([P, E * H], U8, name="w1s_all", align_bytes=64)
-        w2_all = keep.tile([P, E * N], U32, name="w2_all", align_bytes=64)
         w2s_all = keep.tile([P, E * N], U8, name="w2s_all", align_bytes=64)
         xs = keep.tile([P, PASSES, T], U8, name="xs", align_bytes=64)
-        xw = [keep.tile([P, PASSES, HALF], U32, name="xw%d" % h, align_bytes=64) for h in range(2)]
-        gt = [keep.tile([P, G, HALF], F32, name="gt%d" % h, align_bytes=64) for h in range(2)]
 
+        words = PASSES * E * H + E * N + PASSES * T + G * T
+        zeros = stage.tile([P, words], I32, name="zeros", offset=0, align_bytes=64)
         nc.vector.memset(w1s_all[:].bitcast(I32), 0)
-        nc.gpsimd.memset(w2s_all[:].bitcast(I32), 0)
-        nc.vector.memset(xs[:].bitcast(I32), 0)
+        nc.vector.memset(zeros[:, 0 : PASSES * T // 4], 0)
+        nc.vector.tensor_copy(xs[:].rearrange("p s t -> p (s t)").bitcast(I32), zeros[:, 0 : PASSES * T // 4])
+        nc.vector.memset(w2s_all[:].bitcast(I32), 0)
+
+        at = 0
+        w1_all, xw, gt = [], [], []
+        for s in range(PASSES):
+            w1_all.append(stage.tile([P, E * H], U32, name="w1_all%d" % s, align_bytes=64, offset=at))
+            at += 4 * E * H
+        w2_all = stage.tile([P, E * N], U32, name="w2_all", align_bytes=64, offset=at)
+        at += 4 * E * N
+        for h in range(2):
+            xw.append(stage.tile([P, PASSES, HALF], U32, name="xw%d" % h, align_bytes=64, offset=at))
+            at += 4 * PASSES * HALF
+            gt.append(stage.tile([P, G, HALF], F32, name="gt%d" % h, align_bytes=64, offset=at))
+            at += 4 * G * HALF
 
         x_hbm = x_words.rearrange("s p t d -> p s (t d)").bitcast(I32)
         gate_hbm = gate.rearrange("r p t -> p r t")
 
         nc.sync.dma_start(list1[:], offs)
+        nc.sync.dma_start(list2[:], offs2)
         for q in range(4):
             nc.sync.dma_start(w1s_all[:].bitcast(I32)[32 * q : 32 * q + 8, :], w1_scales.bitcast(I32)[:, 4 * q : 4 * q + 4, :])
-        nc.sync.dma_start(w1_all[0][:].bitcast(I32), w1_words[0].rearrange("p m d -> p (m d)").bitcast(I32))
-        nc.sync.dma_start(list2[:], offs2)
-        nc.sync.dma_start(w1_all[1][:].bitcast(I32), w1_words[1].rearrange("p m d -> p (m d)").bitcast(I32))
-        for q in range(4):
-            r0 = 32 * q + W2_ROW
-            nc.gpsimd.dma_start(w2s_all[:].bitcast(I32)[r0 : r0 + 4, :], w2_scales.bitcast(I32)[0, 4 * q : 4 * q + 4, :])
+        for s in range(PASSES):
+            nc.sync.dma_start(w1_all[s][:].bitcast(I32), w1_words[s].rearrange("p m d -> p (m d)").bitcast(I32))
         for q in range(4):
             r0 = 32 * q + X_ROW
             nc.sync.dma_start(
@@ -71,14 +81,15 @@ def tile_moe_wsel_b_relu_p_kernel(
         nc.sync.dma_start(xw[0][:].bitcast(I32), x_hbm[:, :, 0:HALF])
         nc.sync.dma_start(gt[0][:], gate_hbm[:, :, 0:HALF])
         nc.sync.dma_start(xw[1][:].bitcast(I32), x_hbm[:, :, HALF:T])
-        nc.sync.dma_start(w2_all[:].bitcast(I32), w2_words[0].rearrange("p m d -> p (m d)").bitcast(I32))
         nc.sync.dma_start(gt[1][:], gate_hbm[:, :, HALF:T])
+        nc.sync.dma_start(w2_all[:].bitcast(I32), w2_words[0].rearrange("p m d -> p (m d)").bitcast(I32))
+        for q in range(4):
+            r0 = 32 * q + W2_ROW
+            nc.sync.dma_start(w2s_all[:].bitcast(I32)[r0 : r0 + 4, :], w2_scales.bitcast(I32)[0, 4 * q : 4 * q + 4, :])
 
         w1s_sel = keep.tile([P, G * H], U8, name="w1s_sel", align_bytes=64)
         w1s = keep.tile([P, G, PACK, P], U8, name="w1s", align_bytes=64)
         w1 = [[keep.tile([P, PACK, P], U32, name="w1_%d_%d" % (s, r), align_bytes=64) for r in range(G)] for s in range(PASSES)]
-        w2 = keep.tile([P, G * N], U32, name="w2", align_bytes=64)
-        w2s = keep.tile([P, G * N], U8, name="w2s", align_bytes=64)
 
         nc.vector.tensor_copy(w1s_sel[:], w1s_all[:].indirect(list1[:]))
         nc.vector.tensor_copy(w1s[:].rearrange("p r d m -> p r m d"), w1s_sel[:].rearrange("p (r m d) -> p r m d", r=G, d=PACK))
@@ -89,7 +100,6 @@ def tile_moe_wsel_b_relu_p_kernel(
 
         for r in range(G):
             gather_w1(0, r)
-        nc.vector.tensor_copy(w2s[:], w2s_all[:].indirect(list2[:]))
 
         warm = ps2.tile([P, 4 * P], F32, name="warm", tag="acc2")
         for i in range(WARM):
@@ -106,7 +116,7 @@ def tile_moe_wsel_b_relu_p_kernel(
         for r in range(G):
             gather_w1(1, r)
 
-        def layer1(j, r):
+        def layer1(j, r, tag):
             h, c0 = divmod(j * TT, HALF)
             acc = ps1.tile([P, PACK, TT], F32, name="acc", tag="acc1")
             for d in range(PACK):
@@ -120,7 +130,7 @@ def tile_moe_wsel_b_relu_p_kernel(
                         start=(s == 0),
                         stop=(s == PASSES - 1),
                     )
-            hb = work.tile([P, TT, PACK], BF16, name="hb", align_bytes=64)
+            hb = keep.tile([P, TT, PACK], BF16, name="hb", tag=tag, align_bytes=64)
             nc.vector.scalar_tensor_tensor(
                 hb[:],
                 acc[:].rearrange("p d t -> p t d"),
@@ -132,14 +142,17 @@ def tile_moe_wsel_b_relu_p_kernel(
             return hb
 
         def quantise(hb):
-            hq = work.tile([P, TT], U32, name="hq", align_bytes=64, bufs=4)
-            hs = work.tile([P, TT], U8, name="hs", align_bytes=64, bufs=4)
+            hq = work.tile([P, TT], U32, name="hq", align_bytes=64, bufs=8)
+            hs = work.tile([P, TT], U8, name="hs", align_bytes=64, bufs=8)
             nc.vector.quantize_mx(hq[:].bitcast(FP8X4), hs[:], hb[:].rearrange("p t d -> p (t d)"))
             return hq, hs
 
         out_hbm = out.rearrange("(c p) t -> p c t", p=P)
 
+        sel = {}
+
         def pass2(acc, c, r, q):
+            w2, w2s = sel["w2"], sel["w2s"]
             cols = slice(r * N + c * P, r * N + (c + 1) * P)
             nc.tensor.matmul_mx(
                 acc,
@@ -175,11 +188,16 @@ def tile_moe_wsel_b_relu_p_kernel(
         hbs, qs = {}, {}
         for u in range(len(units) + 1):
             if u < len(units):
-                hbs[u] = layer1(*units[u])
-            if u == 2:
-                nc.vector.tensor_copy(w2[:], w2_all[:].indirect(list2[:]))
+                hbs[u] = layer1(*units[u], "hb%d" % u)
             if u >= 1:
                 qs[u - 1] = quantise(hbs[u - 1])
-            if u >= 2 and u % 2 == 0:
+            if u == 3:
+                sel["w2s"] = keep.tile([P, G * N], U8, name="w2s", tag="hb1", align_bytes=64)
+                nc.vector.tensor_copy(sel["w2s"][:], w2s_all[:].indirect(list2[:]))
+            if u == 4:
+                sel["w2"] = keep.tile([P, G * N], U32, name="w2", tag="hb2", align_bytes=64)
+                nc.vector.tensor_copy(sel["w2"][:], w2_all[:].indirect(list2[:]))
+                layer2(0, [qs[0], qs[1]])
+            if u >= 4 and u % 2 == 0:
                 j = u // 2 - 1
                 (layer2_last if j == NT - 1 else layer2)(j, [qs[u - 2], qs[u - 1]])

@@ -1,6 +1,7 @@
 from contextlib import ExitStack
 
 import concourse.mybir as mybir
+from concourse.masks import make_identity
 
 K, T, E, G, H, N = 1024, 512, 4, 2, 512, 256
 FLOPS = 2 * G * T * (K * H + H * N)
@@ -15,15 +16,16 @@ FP8X4 = mybir.dt.float8_e4m3fn_x4
 MAX = mybir.AluOpType.max
 MULT = mybir.AluOpType.mult
 
+RELU = mybir.ActivationFunctionType.Relu
+COPY = mybir.ActivationFunctionType.Copy
+
 P = 128
 PACK = 4
 PASSES = K // (P * PACK)
 TT = 128
 NT = T // TT
 HALF = T // 2
-X_ROW = 12
 W2_ROW = 8
-WARM = 3
 
 
 def tile_moe_wsel_b_relu_p_kernel(
@@ -33,17 +35,17 @@ def tile_moe_wsel_b_relu_p_kernel(
     with ExitStack() as ctx:
         keep = ctx.enter_context(tc.tile_pool(name="keep", bufs=1))
         stage = ctx.enter_context(tc.tile_pool(name="stage", bufs=1))
-        work = ctx.enter_context(tc.tile_pool(name="work", bufs=3))
-        ps1 = ctx.enter_context(tc.psum_pool(name="ps1", bufs=6))
-        ps2 = ctx.enter_context(tc.psum_pool(name="ps2", bufs=2))
+        psum = ctx.enter_context(tc.psum_pool(name="psum", bufs=8))
 
         list1 = keep.tile([P, G * H // 16], U16, name="list1")
         list2 = keep.tile([P, G * N // 16], U16, name="list2")
         w1s_all = keep.tile([P, E * H], U8, name="w1s_all", align_bytes=64)
         w2s_all = keep.tile([P, E * N], U8, name="w2s_all", align_bytes=64)
         xs = keep.tile([P, PASSES, T], U8, name="xs", align_bytes=64)
+        ident = keep.tile([P, P], F32, name="ident")
+        make_identity(nc, ident[:])
 
-        words = PASSES * E * H + E * N + PASSES * T + G * T
+        words = PASSES * E * H + E * N + PASSES * T + G * HALF + 16
         zeros = stage.tile([P, words], I32, name="zeros", offset=0, align_bytes=64)
         nc.vector.memset(w1s_all[:].bitcast(I32), 0)
         nc.vector.memset(zeros[:, 0 : PASSES * T // 4], 0)
@@ -51,153 +53,188 @@ def tile_moe_wsel_b_relu_p_kernel(
         nc.vector.memset(w2s_all[:].bitcast(I32), 0)
 
         at = 0
-        w1_all, xw, gt = [], [], []
+        w1_all, xw = [], []
         for s in range(PASSES):
             w1_all.append(stage.tile([P, E * H], U32, name="w1_all%d" % s, align_bytes=64, offset=at))
             at += 4 * E * H
+        w2_at = at
         w2_all = stage.tile([P, E * N], U32, name="w2_all", align_bytes=64, offset=at)
         at += 4 * E * N
         for h in range(2):
             xw.append(stage.tile([P, PASSES, HALF], U32, name="xw%d" % h, align_bytes=64, offset=at))
             at += 4 * PASSES * HALF
-            gt.append(stage.tile([P, G, HALF], F32, name="gt%d" % h, align_bytes=64, offset=at))
-            at += 4 * G * HALF
+        gate_rows = stage.tile([P, G, HALF], F32, name="gate_rows", align_bytes=64, offset=at)
+        at += 4 * G * HALF
+        gate_cols = stage.tile([P, G, 8], F32, name="gate_cols", align_bytes=64, offset=at)
 
         x_hbm = x_words.rearrange("s p t d -> p s (t d)").bitcast(I32)
-        gate_hbm = gate.rearrange("r p t -> p r t")
+
+        def load_w1(s):
+            nc.sync.dma_start(w1_all[s][:].bitcast(I32), w1_words[s].rearrange("p m d -> p (m d)").bitcast(I32))
 
         nc.sync.dma_start(list1[:], offs)
         nc.sync.dma_start(list2[:], offs2)
         for q in range(4):
             nc.sync.dma_start(w1s_all[:].bitcast(I32)[32 * q : 32 * q + 8, :], w1_scales.bitcast(I32)[:, 4 * q : 4 * q + 4, :])
-        for s in range(PASSES):
-            nc.sync.dma_start(w1_all[s][:].bitcast(I32), w1_words[s].rearrange("p m d -> p (m d)").bitcast(I32))
+        load_w1(0)
+        nc.sync.dma_start(xw[0][:].bitcast(I32), x_hbm[:, :, 0:HALF])
         for q in range(4):
-            r0 = 32 * q + X_ROW
             nc.sync.dma_start(
-                xs[:].bitcast(I32)[r0 : r0 + 4],
+                xs[:].bitcast(I32)[32 * q : 32 * q + 4],
                 x_scales.bitcast(I32)[:, 4 * q : 4 * q + 4, :].rearrange("s j t -> j s t"),
             )
-        nc.sync.dma_start(xw[0][:].bitcast(I32), x_hbm[:, :, 0:HALF])
-        nc.sync.dma_start(gt[0][:], gate_hbm[:, :, 0:HALF])
-        nc.sync.dma_start(xw[1][:].bitcast(I32), x_hbm[:, :, HALF:T])
-        nc.sync.dma_start(gt[1][:], gate_hbm[:, :, HALF:T])
-        nc.sync.dma_start(w2_all[:].bitcast(I32), w2_words[0].rearrange("p m d -> p (m d)").bitcast(I32))
+        load_w1(1)
         for q in range(4):
             r0 = 32 * q + W2_ROW
             nc.sync.dma_start(w2s_all[:].bitcast(I32)[r0 : r0 + 4, :], w2_scales.bitcast(I32)[0, 4 * q : 4 * q + 4, :])
+        nc.sync.dma_start(xw[1][:].bitcast(I32), x_hbm[:, :, HALF:T])
+        with nc.allow_non_contiguous_dma(reason="one gate value a partition"):
+            for r in range(G):
+                nc.sync.dma_start(gate_cols[:, r, 0:2], gate[r, 0, 0:HALF].rearrange("(j p) -> p j", p=P))
+        nc.sync.dma_start(gate_rows[:], gate.rearrange("r p t -> p r t")[:, :, HALF:T])
+        nc.sync.dma_start(w2_all[:].bitcast(I32), w2_words[0].rearrange("p m d -> p (m d)").bitcast(I32))
 
         w1s_sel = keep.tile([P, G * H], U8, name="w1s_sel", align_bytes=64)
         w1s = keep.tile([P, G, PACK, P], U8, name="w1s", align_bytes=64)
         w1 = [[keep.tile([P, PACK, P], U32, name="w1_%d_%d" % (s, r), align_bytes=64) for r in range(G)] for s in range(PASSES)]
 
         nc.vector.tensor_copy(w1s_sel[:], w1s_all[:].indirect(list1[:]))
-        nc.vector.tensor_copy(w1s[:].rearrange("p r d m -> p r m d"), w1s_sel[:].rearrange("p (r m d) -> p r m d", r=G, d=PACK))
+        nc.vector.tensor_copy(
+            w1s[:].rearrange("p r d (b i) -> p r b d i", i=16),
+            w1s_sel[:].rearrange("p (r b i d) -> p r b d i", r=G, i=16, d=PACK),
+        )
 
         def gather_w1(s, r):
             cols = slice(r * H // 16, (r + 1) * H // 16)
             nc.vector.tensor_copy(w1[s][r][:].rearrange("p d m -> p m d"), w1_all[s][:].indirect(list1[:, cols]))
 
-        for r in range(G):
-            gather_w1(0, r)
-
-        warm = ps2.tile([P, 4 * P], F32, name="warm", tag="acc2")
-        for i in range(WARM):
+        def turned_pass(acc, j, r, s):
             nc.tensor.matmul_mx(
-                warm[:],
-                lhsT=w1[0][0][:, 0, :].bitcast(FP8X4),
-                lhsT_scale=w1s[:, 0, 0, :],
-                rhs=w1[0][0][:].rearrange("p d m -> p (d m)").bitcast(FP8X4),
-                rhs_scale=w1s[:, 0].rearrange("p d m -> p (d m)"),
-                start=True,
-                stop=True,
+                acc[:],
+                lhsT=xw[0][:, s, j * TT : (j + 1) * TT].bitcast(FP8X4),
+                lhsT_scale=xs[:, s, j * TT : (j + 1) * TT],
+                rhs=w1[s][r][:].rearrange("p d m -> p (d m)").bitcast(FP8X4),
+                rhs_scale=w1s[4 * s :, r].rearrange("p d m -> p (d m)"),
+                start=(s == 0),
+                stop=(s == PASSES - 1),
             )
 
+        tacc = {}
+        for r in range(G):
+            gather_w1(0, r)
+            for j in range(2):
+                tacc[j, r] = psum.tile([P, H], F32, name="tacc", tag="bank")
+                turned_pass(tacc[j, r], j, r, 0)
         for r in range(G):
             gather_w1(1, r)
+        w2s = stage.tile([P, G * N], U8, name="w2s", align_bytes=64, offset=4 * E * H)
+        nc.vector.tensor_copy(w2s[:], w2s_all[:].indirect(list2[:]))
 
-        def layer1(j, r, tag):
-            h, c0 = divmod(j * TT, HALF)
-            acc = ps1.tile([P, PACK, TT], F32, name="acc", tag="acc1")
+        ht = [keep.tile([P, G, H], BF16, name="ht%d" % j, align_bytes=64) for j in range(2)]
+        hb, hq, hs = {}, {}, {}
+        for j in range(NT):
+            hq[j] = keep.tile([P, G, TT], U32, name="hq%d" % j, align_bytes=64)
+            hs[j] = keep.tile([P, G, TT], U8, name="hs%d" % j, align_bytes=64)
+
+        def turned(j, r):
+            turned_pass(tacc[j, r], j, r, 1)
+            act = keep.tile([P, 2, P, 2], F32, name="act%d_%d" % (j, r))
+            nc.scalar.activation(act[:], tacc[j, r][:].rearrange("t (u e m) -> t u m e", u=2, e=2), RELU)
+            flat = act[:].rearrange("t u m e -> t (u m e)")
+            if j == 0:
+                nc.vector.tensor_scalar(ht[j][:, r, :], flat, gate_cols[:, r, j : j + 1], None, MULT)
+            else:
+                nc.scalar.activation(ht[j][:, r, :], flat, COPY, scale=gate_cols[:, r, j : j + 1])
+
+        def turn_back(j):
+            back = psum.tile([P, G, 2, TT], F32, name="back", tag="bank")
+            for r in range(G):
+                for u in range(2):
+                    nc.tensor.transpose(back[:, r, u, :], ht[j][:, r, :].bitcast(F32)[:, u * P : (u + 1) * P], ident[:])
+            hb[j] = keep.tile([P, G, TT * PACK], BF16, name="hb%d" % j, align_bytes=64)
+            nc.scalar.copy(hb[j][:].bitcast(F32).rearrange("p r (t u) -> p r t u", u=2), back[:].rearrange("p r u t -> p r t u"))
+
+        def direct(j, r, dst):
+            c0 = j * TT - HALF
+            acc = psum.tile([P, PACK, TT], F32, name="acc", tag="bank")
             for d in range(PACK):
                 for s in range(PASSES):
                     nc.tensor.matmul_mx(
                         acc[:, d, :],
                         lhsT=w1[s][r][:, d, :].bitcast(FP8X4),
                         lhsT_scale=w1s[4 * s :, r, d, :],
-                        rhs=xw[h][:, s, c0 : c0 + TT].bitcast(FP8X4),
-                        rhs_scale=xs[X_ROW:, s, j * TT : (j + 1) * TT],
+                        rhs=xw[1][:, s, c0 : c0 + TT].bitcast(FP8X4),
+                        rhs_scale=xs[:, s, j * TT : (j + 1) * TT],
                         start=(s == 0),
                         stop=(s == PASSES - 1),
                     )
-            hb = keep.tile([P, TT, PACK], BF16, name="hb", tag=tag, align_bytes=64)
             nc.vector.scalar_tensor_tensor(
-                hb[:],
+                dst.rearrange("p (t d) -> p t d", d=PACK),
                 acc[:].rearrange("p d t -> p t d"),
                 0.0,
-                gt[h][:, r, c0 : c0 + TT].unsqueeze(2).to_broadcast([P, TT, PACK]),
+                gate_rows[:, r, c0 : c0 + TT].unsqueeze(2).to_broadcast([P, TT, PACK]),
                 MAX,
                 MULT,
             )
-            return hb
 
-        def quantise(hb):
-            hq = work.tile([P, TT], U32, name="hq", align_bytes=64, bufs=8)
-            hs = work.tile([P, TT], U8, name="hs", align_bytes=64, bufs=8)
-            nc.vector.quantize_mx(hq[:].bitcast(FP8X4), hs[:], hb[:].rearrange("p t d -> p (t d)"))
-            return hq, hs
+        def quantise_both(j):
+            nc.vector.quantize_mx(
+                hq[j][:].rearrange("p r t -> p (r t)").bitcast(FP8X4),
+                hs[j][:].rearrange("p r t -> p (r t)"),
+                hb[j][:].rearrange("p r c -> p (r c)"),
+            )
 
         out_hbm = out.rearrange("(c p) t -> p c t", p=P)
 
-        sel = {}
-
-        def pass2(acc, c, r, q):
-            w2, w2s = sel["w2"], sel["w2s"]
+        def pass2(acc, c, r, j):
             cols = slice(r * N + c * P, r * N + (c + 1) * P)
             nc.tensor.matmul_mx(
                 acc,
                 lhsT=w2[:, cols].bitcast(FP8X4),
                 lhsT_scale=w2s[W2_ROW:, cols],
-                rhs=q[0][:].bitcast(FP8X4),
-                rhs_scale=q[1][:],
+                rhs=hq[j][:, r, :].bitcast(FP8X4),
+                rhs_scale=hs[j][:, r, :],
                 start=(r == 0),
                 stop=(r == G - 1),
             )
 
-        def layer2(j, qs):
-            acc = ps2.tile([P, 2, TT], F32, name="acc2", tag="acc2")
+        def layer2(j, engine_copy, queue):
+            acc = psum.tile([P, 2, TT], F32, name="acc2", tag="bank")
             for c in range(2):
                 for r in range(G):
-                    pass2(acc[:, c, :], c, r, qs[r])
-            res = work.tile([P, 2, TT], F32, name="res")
-            nc.scalar.copy(res[:], acc[:])
-            nc.sync.dma_start(out_hbm[:, :, j * TT : (j + 1) * TT], res[:])
+                    pass2(acc[:, c, :], c, r, j)
+            res = keep.tile([P, 2, TT], F32, name="res%d" % j)
+            engine_copy(res[:], acc[:])
+            queue.dma_start(out_hbm[:, :, j * TT : (j + 1) * TT], res[:])
 
-        def layer2_last(j, qs):
-            accs = [ps1.tile([P, TT], F32, name="acc_last%d" % c, tag="acc1") for c in range(2)]
-            for r in range(G):
-                for c in range(2):
-                    pass2(accs[c][:], c, r, qs[r])
-            res = [keep.tile([P, TT], F32, name="res_last%d" % c) for c in range(2)]
-            nc.scalar.copy(res[0][:], accs[0][:])
-            nc.vector.tensor_copy(res[1][:], accs[1][:])
-            nc.scalar.dma_start(out_hbm[:, 0, j * TT : (j + 1) * TT], res[0][:])
-            nc.sync.dma_start(out_hbm[:, 1, j * TT : (j + 1) * TT], res[1][:])
-
-        units = [(j, r) for j in range(NT) for r in range(G)]
-        hbs, qs = {}, {}
-        for u in range(len(units) + 1):
-            if u < len(units):
-                hbs[u] = layer1(*units[u], "hb%d" % u)
-            if u >= 1:
-                qs[u - 1] = quantise(hbs[u - 1])
-            if u == 3:
-                sel["w2s"] = keep.tile([P, G * N], U8, name="w2s", tag="hb1", align_bytes=64)
-                nc.vector.tensor_copy(sel["w2s"][:], w2s_all[:].indirect(list2[:]))
-            if u == 4:
-                sel["w2"] = keep.tile([P, G * N], U32, name="w2", tag="hb2", align_bytes=64)
-                nc.vector.tensor_copy(sel["w2"][:], w2_all[:].indirect(list2[:]))
-                layer2(0, [qs[0], qs[1]])
-            if u >= 4 and u % 2 == 0:
-                j = u // 2 - 1
-                (layer2_last if j == NT - 1 else layer2)(j, [qs[u - 2], qs[u - 1]])
+        hb[2] = keep.tile([P, G, TT * PACK], BF16, name="hb2", tag="late_a", align_bytes=64)
+        turned(0, 0)
+        direct(2, 0, hb[2][:, 0, :])
+        turned(0, 1)
+        turned(1, 0)
+        direct(2, 1, hb[2][:, 1, :])
+        turned(1, 1)
+        turn_back(0)
+        quantise_both(2)
+        w2 = keep.tile([P, G * N], U32, name="w2", tag="late_a", align_bytes=64)
+        nc.vector.tensor_copy(w2[:], w2_all[:].indirect(list2[:]))
+        hb3a = stage.tile([P, TT * PACK], BF16, name="hb3a", align_bytes=64, offset=w2_at)
+        direct(3, 0, hb3a[:])
+        quantise_both(0)
+        hb3b = keep.tile([P, TT * PACK], BF16, name="hb3b", align_bytes=64)
+        direct(3, 1, hb3b[:])
+        turn_back(1)
+        layer2(2, nc.scalar.copy, nc.sync)
+        layer2(0, nc.scalar.copy, nc.sync)
+        last = [psum.tile([P, TT], F32, name="last%d" % c, tag="bank") for c in range(2)]
+        nc.vector.quantize_mx(hq[3][:, 0, :].bitcast(FP8X4), hs[3][:, 0, :], hb3a[:])
+        for c in range(2):
+            pass2(last[c][:], c, 0, 3)
+        quantise_both(1)
+        layer2(1, nc.scalar.copy, nc.scalar)
+        nc.vector.quantize_mx(hq[3][:, 1, :].bitcast(FP8X4), hs[3][:, 1, :], hb3b[:])
+        res = keep.tile([P, 2, TT], F32, name="res3")
+        for c in range(2):
+            pass2(last[c][:], c, 1, 3)
+            nc.vector.tensor_copy(res[:, c, :], last[c][:])
+        nc.sync.dma_start(out_hbm[:, :, 3 * TT : 4 * TT], res[:])

@@ -15,17 +15,21 @@ U8 = mybir.dt.uint8
 FP8X4 = mybir.dt.float8_e4m3fn_x4
 MAX = mybir.AluOpType.max
 MULT = mybir.AluOpType.mult
-
 RELU = mybir.ActivationFunctionType.Relu
 COPY = mybir.ActivationFunctionType.Copy
 
 P = 128
 PACK = 4
 PASSES = K // (P * PACK)
+QUADRANTS = 4
+PER_COLUMN = 16
 TT = 128
-NT = T // TT
 HALF = T // 2
+TURNED = HALF // TT
+OUT_TILES = N // P
+W1_ROWS = 4
 W2_ROW = 8
+ALIGN = 64
 
 
 def tile_moe_wsel_b_relu_p_kernel(
@@ -37,35 +41,36 @@ def tile_moe_wsel_b_relu_p_kernel(
         stage = ctx.enter_context(tc.tile_pool(name="stage", bufs=1))
         psum = ctx.enter_context(tc.psum_pool(name="psum", bufs=8))
 
-        list1 = keep.tile([P, G * H // 16], U16, name="list1")
-        list2 = keep.tile([P, G * N // 16], U16, name="list2")
-        w1s_all = keep.tile([P, E * H], U8, name="w1s_all", align_bytes=64)
-        w2s_all = keep.tile([P, E * N], U8, name="w2s_all", align_bytes=64)
-        xs = keep.tile([P, PASSES, T], U8, name="xs", align_bytes=64)
+        list1 = keep.tile([P, G * H // PER_COLUMN], U16, name="list1")
+        list2 = keep.tile([P, G * N // PER_COLUMN], U16, name="list2")
+        w1s_all = keep.tile([P, E * H], U8, name="w1s_all", align_bytes=ALIGN)
+        w2s_all = keep.tile([P, E * N], U8, name="w2s_all", align_bytes=ALIGN)
+        xs = keep.tile([P, PASSES, T], U8, name="xs", align_bytes=ALIGN)
         ident = keep.tile([P, P], F32, name="ident")
         make_identity(nc, ident[:])
 
-        words = PASSES * E * H + E * N + PASSES * T + G * HALF + 16
-        zeros = stage.tile([P, words], I32, name="zeros", offset=0, align_bytes=64)
+        stage_words = PASSES * E * H + E * N + PASSES * T + G * HALF + TT
+        xs_words = PASSES * T // 4
+        zeros = stage.tile([P, stage_words], I32, name="zeros", offset=0, align_bytes=ALIGN)
         nc.vector.memset(w1s_all[:].bitcast(I32), 0)
-        nc.vector.memset(zeros[:, 0 : PASSES * T // 4], 0)
-        nc.vector.tensor_copy(xs[:].rearrange("p s t -> p (s t)").bitcast(I32), zeros[:, 0 : PASSES * T // 4])
+        nc.vector.memset(zeros[:, 0:xs_words], 0)
+        nc.vector.tensor_copy(xs[:].rearrange("p s t -> p (s t)").bitcast(I32), zeros[:, 0:xs_words])
         nc.vector.memset(w2s_all[:].bitcast(I32), 0)
 
-        at = 0
-        w1_all, xw = [], []
-        for s in range(PASSES):
-            w1_all.append(stage.tile([P, E * H], U32, name="w1_all%d" % s, align_bytes=64, offset=at))
-            at += 4 * E * H
-        w2_at = at
-        w2_all = stage.tile([P, E * N], U32, name="w2_all", align_bytes=64, offset=at)
-        at += 4 * E * N
-        for h in range(2):
-            xw.append(stage.tile([P, PASSES, HALF], U32, name="xw%d" % h, align_bytes=64, offset=at))
-            at += 4 * PASSES * HALF
-        gate_rows = stage.tile([P, G, HALF], F32, name="gate_rows", align_bytes=64, offset=at)
-        at += 4 * G * HALF
-        gate_cols = stage.tile([P, G, 8], F32, name="gate_cols", align_bytes=64, offset=at)
+        w1_at = [4 * E * H * s for s in range(PASSES)]
+        w2_at = 4 * E * H * PASSES
+        x_at = [w2_at + 4 * E * N + 4 * PASSES * HALF * road for road in range(2)]
+        gate_rows_at = x_at[1] + 4 * PASSES * HALF
+        gate_few_at = gate_rows_at + 4 * G * HALF
+        w1_all = [
+            stage.tile([P, E * H], U32, name="w1_all%d" % s, align_bytes=ALIGN, offset=w1_at[s]) for s in range(PASSES)
+        ]
+        w2_all = stage.tile([P, E * N], U32, name="w2_all", align_bytes=ALIGN, offset=w2_at)
+        x_turned = stage.tile([P, PASSES, HALF], U32, name="x_turned", align_bytes=ALIGN, offset=x_at[0])
+        x_direct = stage.tile([P, PASSES, HALF], U32, name="x_direct", align_bytes=ALIGN, offset=x_at[1])
+        gate_rows = stage.tile([P, G, HALF], F32, name="gate_rows", align_bytes=ALIGN, offset=gate_rows_at)
+        gate_few = stage.tile([P, TT], F32, name="gate_few", align_bytes=ALIGN, offset=gate_few_at)
+        nc.gpsimd.memset(gate_few[:], 0.0)
 
         x_hbm = x_words.rearrange("s p t d -> p s (t d)").bitcast(I32)
 
@@ -74,105 +79,117 @@ def tile_moe_wsel_b_relu_p_kernel(
 
         nc.sync.dma_start(list1[:], offs)
         nc.sync.dma_start(list2[:], offs2)
-        for q in range(4):
-            nc.sync.dma_start(w1s_all[:].bitcast(I32)[32 * q : 32 * q + 8, :], w1_scales.bitcast(I32)[:, 4 * q : 4 * q + 4, :])
+        for q in range(QUADRANTS):
+            nc.sync.dma_start(
+                w1s_all[:].bitcast(I32)[32 * q : 32 * q + W1_ROWS * PASSES, :],
+                w1_scales.bitcast(I32)[:, 4 * q : 4 * q + 4, :],
+            )
         load_w1(0)
-        nc.sync.dma_start(xw[0][:].bitcast(I32), x_hbm[:, :, 0:HALF])
-        for q in range(4):
+        nc.sync.dma_start(x_turned[:].bitcast(I32), x_hbm[:, :, 0:HALF])
+        for q in range(QUADRANTS):
             nc.sync.dma_start(
                 xs[:].bitcast(I32)[32 * q : 32 * q + 4],
                 x_scales.bitcast(I32)[:, 4 * q : 4 * q + 4, :].rearrange("s j t -> j s t"),
             )
+        nc.sync.dma_start(gate_few[0 : G * TURNED, :], gate[:, 0, 0:HALF].rearrange("r (j t) -> r j t", t=TT))
         load_w1(1)
-        for q in range(4):
-            r0 = 32 * q + W2_ROW
-            nc.sync.dma_start(w2s_all[:].bitcast(I32)[r0 : r0 + 4, :], w2_scales.bitcast(I32)[0, 4 * q : 4 * q + 4, :])
-        nc.sync.dma_start(xw[1][:].bitcast(I32), x_hbm[:, :, HALF:T])
-        with nc.allow_non_contiguous_dma(reason="one gate value a partition"):
-            for r in range(G):
-                nc.sync.dma_start(gate_cols[:, r, 0:2], gate[r, 0, 0:HALF].rearrange("(j p) -> p j", p=P))
+        for q in range(QUADRANTS):
+            nc.sync.dma_start(
+                w2s_all[:].bitcast(I32)[32 * q + W2_ROW : 32 * q + W2_ROW + 4, :],
+                w2_scales.bitcast(I32)[0, 4 * q : 4 * q + 4, :],
+            )
+        nc.sync.dma_start(x_direct[:].bitcast(I32), x_hbm[:, :, HALF:T])
         nc.sync.dma_start(gate_rows[:], gate.rearrange("r p t -> p r t")[:, :, HALF:T])
         nc.sync.dma_start(w2_all[:].bitcast(I32), w2_words[0].rearrange("p m d -> p (m d)").bitcast(I32))
 
-        w1s_sel = keep.tile([P, G * H], U8, name="w1s_sel", align_bytes=64)
-        w1s = keep.tile([P, G, PACK, P], U8, name="w1s", align_bytes=64)
-        w1 = [[keep.tile([P, PACK, P], U32, name="w1_%d_%d" % (s, r), align_bytes=64) for r in range(G)] for s in range(PASSES)]
-
-        nc.vector.tensor_copy(w1s_sel[:], w1s_all[:].indirect(list1[:]))
+        w1s_listed = keep.tile([P, G * H], U8, name="w1s_listed", align_bytes=ALIGN)
+        w1s = keep.tile([P, G, PACK, P], U8, name="w1s", align_bytes=ALIGN)
+        w1 = [
+            [keep.tile([P, PACK, P], U32, name="w1_%d_%d" % (s, r), align_bytes=ALIGN) for r in range(G)]
+            for s in range(PASSES)
+        ]
+        nc.vector.tensor_copy(w1s_listed[:], w1s_all[:].indirect(list1[:]))
         nc.vector.tensor_copy(
-            w1s[:].rearrange("p r d (b i) -> p r b d i", i=16),
-            w1s_sel[:].rearrange("p (r b i d) -> p r b d i", r=G, i=16, d=PACK),
+            w1s[:].rearrange("p r d (a m) -> p r a d m", m=16),
+            w1s_listed[:].rearrange("p (r a m d) -> p r a d m", r=G, m=16, d=PACK),
         )
 
         def gather_w1(s, r):
-            cols = slice(r * H // 16, (r + 1) * H // 16)
-            nc.vector.tensor_copy(w1[s][r][:].rearrange("p d m -> p m d"), w1_all[s][:].indirect(list1[:, cols]))
+            entries = slice(r * H // PER_COLUMN, (r + 1) * H // PER_COLUMN)
+            nc.vector.tensor_copy(w1[s][r][:].rearrange("p d m -> p m d"), w1_all[s][:].indirect(list1[:, entries]))
 
-        def turned_pass(acc, j, r, s):
+        def turned_pass(j, r, s):
             nc.tensor.matmul_mx(
-                acc[:],
-                lhsT=xw[0][:, s, j * TT : (j + 1) * TT].bitcast(FP8X4),
+                turned_sum[j, r][:],
+                lhsT=x_turned[:, s, j * TT : (j + 1) * TT].bitcast(FP8X4),
                 lhsT_scale=xs[:, s, j * TT : (j + 1) * TT],
                 rhs=w1[s][r][:].rearrange("p d m -> p (d m)").bitcast(FP8X4),
-                rhs_scale=w1s[4 * s :, r].rearrange("p d m -> p (d m)"),
+                rhs_scale=w1s[W1_ROWS * s :, r].rearrange("p d m -> p (d m)"),
                 start=(s == 0),
                 stop=(s == PASSES - 1),
             )
 
-        tacc = {}
+        gate_turned = psum.tile([P, P], F32, name="gate_turned", tag="bank")
+        nc.tensor.transpose(gate_turned[:], gate_few[:], ident[:])
+        gate_cols = keep.tile([P, G, TURNED], F32, name="gate_cols")
+        nc.scalar.copy(gate_cols[:].rearrange("t r j -> t (r j)"), gate_turned[:, 0 : G * TURNED])
+
+        turned_sum = {}
         for r in range(G):
             gather_w1(0, r)
-            for j in range(2):
-                tacc[j, r] = psum.tile([P, H], F32, name="tacc", tag="bank")
-                turned_pass(tacc[j, r], j, r, 0)
+            for j in range(TURNED):
+                turned_sum[j, r] = psum.tile([P, H], F32, name="turned_sum", tag="bank")
+                turned_pass(j, r, 0)
         for r in range(G):
             gather_w1(1, r)
-        w2s = stage.tile([P, G * N], U8, name="w2s", align_bytes=64, offset=4 * E * H)
+        w2s = stage.tile([P, G * N], U8, name="w2s", align_bytes=ALIGN, offset=w1_at[1])
         nc.vector.tensor_copy(w2s[:], w2s_all[:].indirect(list2[:]))
 
-        ht = [keep.tile([P, G, H], BF16, name="ht%d" % j, align_bytes=64) for j in range(2)]
-        hb, hq, hs = {}, {}, {}
-        for j in range(NT):
-            hq[j] = keep.tile([P, G, TT], U32, name="hq%d" % j, align_bytes=64)
-            hs[j] = keep.tile([P, G, TT], U8, name="hs%d" % j, align_bytes=64)
+        h_turned = [keep.tile([P, G, H], BF16, name="h_turned%d" % j, align_bytes=ALIGN) for j in range(TURNED)]
+        h, hq, hs = {}, {}, {}
+        for j in range(T // TT):
+            hq[j] = keep.tile([P, G, TT], U32, name="hq%d" % j, align_bytes=ALIGN)
+            hs[j] = keep.tile([P, G, TT], U8, name="hs%d" % j, align_bytes=ALIGN)
 
-        def turned(j, r):
-            turned_pass(tacc[j, r], j, r, 1)
-            act = keep.tile([P, 2, P, 2], F32, name="act%d_%d" % (j, r))
-            nc.scalar.activation(act[:], tacc[j, r][:].rearrange("t (u e m) -> t u m e", u=2, e=2), RELU)
-            flat = act[:].rearrange("t u m e -> t (u m e)")
-            if j == 0:
-                nc.vector.tensor_scalar(ht[j][:, r, :], flat, gate_cols[:, r, j : j + 1], None, MULT)
+        def turned(j, r, gate_on_vector):
+            turned_pass(j, r, PASSES - 1)
+            relu = keep.tile([P, 2, P, 2], F32, name="relu", tag="relu%d%d" % (j, r), align_bytes=ALIGN)
+            nc.scalar.activation(relu[:], turned_sum[j, r][:].rearrange("t (u e m) -> t u m e", u=2, e=2), RELU)
+            relu_flat = relu[:].rearrange("t u m e -> t (u m e)")
+            gate_col = gate_cols[:, r, j : j + 1]
+            if gate_on_vector:
+                nc.vector.tensor_scalar(h_turned[j][:, r, :], relu_flat, gate_col, None, MULT)
             else:
-                nc.scalar.activation(ht[j][:, r, :], flat, COPY, scale=gate_cols[:, r, j : j + 1])
+                nc.scalar.activation(h_turned[j][:, r, :], relu_flat, COPY, scale=gate_col)
 
         def turn_back(j):
             back = psum.tile([P, G, 2, TT], F32, name="back", tag="bank")
             for r in range(G):
                 for u in range(2):
-                    nc.tensor.transpose(back[:, r, u, :], ht[j][:, r, :].bitcast(F32)[:, u * P : (u + 1) * P], ident[:])
-            hb[j] = keep.tile([P, G, TT * PACK], BF16, name="hb%d" % j, align_bytes=64)
-            nc.scalar.copy(hb[j][:].bitcast(F32).rearrange("p r (t u) -> p r t u", u=2), back[:].rearrange("p r u t -> p r t u"))
+                    pairs = h_turned[j][:, r, :].bitcast(F32)[:, u * P : (u + 1) * P]
+                    nc.tensor.transpose(back[:, r, u, :], pairs, ident[:])
+            h[j] = keep.tile([P, G, TT * PACK], BF16, name="h%d" % j, align_bytes=ALIGN)
+            nc.scalar.copy(h[j][:].bitcast(F32).rearrange("p r (t u) -> p r t u", u=2), back[:].rearrange("p r u t -> p r t u"))
 
         def direct(j, r, dst):
-            c0 = j * TT - HALF
-            acc = psum.tile([P, PACK, TT], F32, name="acc", tag="bank")
+            tokens = slice(j * TT - HALF, (j + 1) * TT - HALF)
+            direct_sum = psum.tile([P, PACK, TT], F32, name="direct_sum", tag="bank")
             for d in range(PACK):
                 for s in range(PASSES):
                     nc.tensor.matmul_mx(
-                        acc[:, d, :],
+                        direct_sum[:, d, :],
                         lhsT=w1[s][r][:, d, :].bitcast(FP8X4),
-                        lhsT_scale=w1s[4 * s :, r, d, :],
-                        rhs=xw[1][:, s, c0 : c0 + TT].bitcast(FP8X4),
+                        lhsT_scale=w1s[W1_ROWS * s :, r, d, :],
+                        rhs=x_direct[:, s, tokens].bitcast(FP8X4),
                         rhs_scale=xs[:, s, j * TT : (j + 1) * TT],
                         start=(s == 0),
                         stop=(s == PASSES - 1),
                     )
             nc.vector.scalar_tensor_tensor(
                 dst.rearrange("p (t d) -> p t d", d=PACK),
-                acc[:].rearrange("p d t -> p t d"),
+                direct_sum[:].rearrange("p d t -> p t d"),
                 0.0,
-                gate_rows[:, r, c0 : c0 + TT].unsqueeze(2).to_broadcast([P, TT, PACK]),
+                gate_rows[:, r, tokens].unsqueeze(2).to_broadcast([P, TT, PACK]),
                 MAX,
                 MULT,
             )
@@ -181,15 +198,15 @@ def tile_moe_wsel_b_relu_p_kernel(
             nc.vector.quantize_mx(
                 hq[j][:].rearrange("p r t -> p (r t)").bitcast(FP8X4),
                 hs[j][:].rearrange("p r t -> p (r t)"),
-                hb[j][:].rearrange("p r c -> p (r c)"),
+                h[j][:].rearrange("p r c -> p (r c)"),
             )
 
         out_hbm = out.rearrange("(c p) t -> p c t", p=P)
 
-        def pass2(acc, c, r, j):
+        def second_pass(dst, c, r, j):
             cols = slice(r * N + c * P, r * N + (c + 1) * P)
             nc.tensor.matmul_mx(
-                acc,
+                dst,
                 lhsT=w2[:, cols].bitcast(FP8X4),
                 lhsT_scale=w2s[W2_ROW:, cols],
                 rhs=hq[j][:, r, :].bitcast(FP8X4),
@@ -198,43 +215,44 @@ def tile_moe_wsel_b_relu_p_kernel(
                 stop=(r == G - 1),
             )
 
-        def layer2(j, engine_copy, queue):
-            acc = psum.tile([P, 2, TT], F32, name="acc2", tag="bank")
-            for c in range(2):
+        def second_layer(j, queue):
+            out_sum = psum.tile([P, OUT_TILES, TT], F32, name="out_sum", tag="bank")
+            for c in range(OUT_TILES):
                 for r in range(G):
-                    pass2(acc[:, c, :], c, r, j)
-            res = keep.tile([P, 2, TT], F32, name="res%d" % j)
-            engine_copy(res[:], acc[:])
-            queue.dma_start(out_hbm[:, :, j * TT : (j + 1) * TT], res[:])
+                    second_pass(out_sum[:, c, :], c, r, j)
+            result = keep.tile([P, OUT_TILES, TT], F32, name="result%d" % j)
+            nc.scalar.copy(result[:], out_sum[:])
+            queue.dma_start(out_hbm[:, :, j * TT : (j + 1) * TT], result[:])
 
-        hb[2] = keep.tile([P, G, TT * PACK], BF16, name="hb2", tag="late_a", align_bytes=64)
-        turned(0, 0)
-        direct(2, 0, hb[2][:, 0, :])
-        turned(0, 1)
-        turned(1, 0)
-        direct(2, 1, hb[2][:, 1, :])
-        turned(1, 1)
-        turn_back(0)
-        quantise_both(2)
-        w2 = keep.tile([P, G * N], U32, name="w2", tag="late_a", align_bytes=64)
+        h[2] = keep.tile([P, G, TT * PACK], BF16, name="h2", align_bytes=ALIGN)
+        turned(0, 0, gate_on_vector=True)
+        turned(1, 0, gate_on_vector=False)
+        direct(2, 0, h[2][:, 0, :])
+        w2 = keep.tile([P, G * N], U32, name="w2", tag="relu10", align_bytes=ALIGN)
         nc.vector.tensor_copy(w2[:], w2_all[:].indirect(list2[:]))
-        hb3a = stage.tile([P, TT * PACK], BF16, name="hb3a", align_bytes=64, offset=w2_at)
-        direct(3, 0, hb3a[:])
-        quantise_both(0)
-        hb3b = keep.tile([P, TT * PACK], BF16, name="hb3b", align_bytes=64)
-        direct(3, 1, hb3b[:])
+        turned(0, 1, gate_on_vector=True)
+        turned(1, 1, gate_on_vector=False)
+        direct(2, 1, h[2][:, 1, :])
+        turn_back(0)
+        h3_first = stage.tile([P, TT * PACK], BF16, name="h3_first", align_bytes=ALIGN, offset=w2_at)
+        direct(3, 0, h3_first[:])
         turn_back(1)
-        layer2(2, nc.scalar.copy, nc.sync)
-        layer2(0, nc.scalar.copy, nc.sync)
-        last = [psum.tile([P, TT], F32, name="last%d" % c, tag="bank") for c in range(2)]
-        nc.vector.quantize_mx(hq[3][:, 0, :].bitcast(FP8X4), hs[3][:, 0, :], hb3a[:])
-        for c in range(2):
-            pass2(last[c][:], c, 0, 3)
+        quantise_both(2)
+        h3_second = keep.tile([P, TT * PACK], BF16, name="h3_second", align_bytes=ALIGN)
+        direct(3, 1, h3_second[:])
+        quantise_both(0)
+        second_layer(2, nc.sync)
+        second_layer(0, nc.sync)
+
+        last_sum = [psum.tile([P, TT], F32, name="last_sum%d" % c, tag="bank") for c in range(OUT_TILES)]
+        nc.vector.quantize_mx(hq[3][:, 0, :].bitcast(FP8X4), hs[3][:, 0, :], h3_first[:])
+        for c in range(OUT_TILES):
+            second_pass(last_sum[c][:], c, 0, 3)
         quantise_both(1)
-        layer2(1, nc.scalar.copy, nc.scalar)
-        nc.vector.quantize_mx(hq[3][:, 1, :].bitcast(FP8X4), hs[3][:, 1, :], hb3b[:])
-        res = keep.tile([P, 2, TT], F32, name="res3")
-        for c in range(2):
-            pass2(last[c][:], c, 1, 3)
-            nc.vector.tensor_copy(res[:, c, :], last[c][:])
-        nc.sync.dma_start(out_hbm[:, :, 3 * TT : 4 * TT], res[:])
+        second_layer(1, nc.scalar)
+        nc.vector.quantize_mx(hq[3][:, 1, :].bitcast(FP8X4), hs[3][:, 1, :], h3_second[:])
+        last_result = keep.tile([P, OUT_TILES, TT], F32, name="last_result")
+        for c in range(OUT_TILES):
+            second_pass(last_sum[c][:], c, 1, 3)
+            nc.vector.tensor_copy(last_result[:, c, :], last_sum[c][:])
+        nc.sync.dma_start(out_hbm[:, :, 3 * TT : 4 * TT], last_result[:])

@@ -15,8 +15,10 @@ U8 = mybir.dt.uint8
 FP8X4 = mybir.dt.float8_e4m3fn_x4
 MAX = mybir.AluOpType.max
 MULT = mybir.AluOpType.mult
+ADD = mybir.AluOpType.add
 RELU = mybir.ActivationFunctionType.Relu
-COPY = mybir.ActivationFunctionType.Copy
+ABS = mybir.ActivationFunctionType.Abs
+SIGN = mybir.ActivationFunctionType.Sign
 
 P = 128
 PACK = 4
@@ -24,8 +26,9 @@ PASSES = K // (P * PACK)
 QUADRANTS = 4
 PER_COLUMN = 16
 TT = 128
+TILES = T // TT
 HALF = T // 2
-TURNED = HALF // TT
+TURNED = 3
 OUT_TILES = N // P
 W1_ROWS = 4
 W2_ROW = 8
@@ -49,7 +52,7 @@ def tile_moe_wsel_b_relu_p_kernel(
         ident = keep.tile([P, P], F32, name="ident")
         make_identity(nc, ident[:])
 
-        stage_words = PASSES * E * H + E * N + PASSES * T + G * HALF + TT
+        stage_words = PASSES * E * H + E * N + PASSES * HALF + G * HALF + TT
         xs_words = PASSES * T // 4
         zeros = stage.tile([P, stage_words], I32, name="zeros", offset=0, align_bytes=ALIGN)
         nc.vector.memset(w1s_all[:].bitcast(I32), 0)
@@ -59,48 +62,49 @@ def tile_moe_wsel_b_relu_p_kernel(
 
         w1_at = [4 * E * H * s for s in range(PASSES)]
         w2_at = 4 * E * H * PASSES
-        x_at = [w2_at + 4 * E * N + 4 * PASSES * HALF * road for road in range(2)]
-        gate_rows_at = x_at[1] + 4 * PASSES * HALF
+        x_at = w2_at + 4 * E * N
+        gate_rows_at = x_at + 4 * PASSES * HALF
         gate_few_at = gate_rows_at + 4 * G * HALF
         w1_all = [
             stage.tile([P, E * H], U32, name="w1_all%d" % s, align_bytes=ALIGN, offset=w1_at[s]) for s in range(PASSES)
         ]
         w2_all = stage.tile([P, E * N], U32, name="w2_all", align_bytes=ALIGN, offset=w2_at)
-        x_turned = stage.tile([P, PASSES, HALF], U32, name="x_turned", align_bytes=ALIGN, offset=x_at[0])
-        x_direct = stage.tile([P, PASSES, HALF], U32, name="x_direct", align_bytes=ALIGN, offset=x_at[1])
+        x = [
+            keep.tile([P, PASSES, HALF], U32, name="x0", align_bytes=ALIGN),
+            stage.tile([P, PASSES, HALF], U32, name="x1", align_bytes=ALIGN, offset=x_at),
+        ]
         gate_rows = stage.tile([P, G, HALF], F32, name="gate_rows", align_bytes=ALIGN, offset=gate_rows_at)
         gate_few = stage.tile([P, TT], F32, name="gate_few", align_bytes=ALIGN, offset=gate_few_at)
         nc.gpsimd.memset(gate_few[:], 0.0)
 
+        def load_words(dst, src):
+            nc.sync.dma_start(dst[:].bitcast(I32), src.rearrange("p m d -> p (m d)").bitcast(I32))
+
         x_hbm = x_words.rearrange("s p t d -> p s (t d)").bitcast(I32)
-
-        def load_w1(s):
-            nc.sync.dma_start(w1_all[s][:].bitcast(I32), w1_words[s].rearrange("p m d -> p (m d)").bitcast(I32))
-
         nc.sync.dma_start(list1[:], offs)
+        nc.sync.dma_start(x[0][:].bitcast(I32), x_hbm[:, :, 0:HALF])
         nc.sync.dma_start(list2[:], offs2)
         for q in range(QUADRANTS):
             nc.sync.dma_start(
                 w1s_all[:].bitcast(I32)[32 * q : 32 * q + W1_ROWS * PASSES, :],
                 w1_scales.bitcast(I32)[:, 4 * q : 4 * q + 4, :],
             )
-        load_w1(0)
-        nc.sync.dma_start(x_turned[:].bitcast(I32), x_hbm[:, :, 0:HALF])
+        load_words(w1_all[0], w1_words[0])
         for q in range(QUADRANTS):
             nc.sync.dma_start(
                 xs[:].bitcast(I32)[32 * q : 32 * q + 4],
                 x_scales.bitcast(I32)[:, 4 * q : 4 * q + 4, :].rearrange("s j t -> j s t"),
             )
-        nc.sync.dma_start(gate_few[0 : G * TURNED, :], gate[:, 0, 0:HALF].rearrange("r (j t) -> r j t", t=TT))
-        load_w1(1)
+        nc.sync.dma_start(gate_few[0 : G * TURNED, :], gate[:, 0, 0 : TURNED * TT].rearrange("r (j t) -> r j t", t=TT))
+        load_words(w1_all[1], w1_words[1])
+        nc.sync.dma_start(x[1][:].bitcast(I32), x_hbm[:, :, HALF:T])
+        nc.sync.dma_start(gate_rows[:], gate.rearrange("r p t -> p r t")[:, :, HALF:T])
         for q in range(QUADRANTS):
             nc.sync.dma_start(
                 w2s_all[:].bitcast(I32)[32 * q + W2_ROW : 32 * q + W2_ROW + 4, :],
                 w2_scales.bitcast(I32)[0, 4 * q : 4 * q + 4, :],
             )
-        nc.sync.dma_start(x_direct[:].bitcast(I32), x_hbm[:, :, HALF:T])
-        nc.sync.dma_start(gate_rows[:], gate.rearrange("r p t -> p r t")[:, :, HALF:T])
-        nc.sync.dma_start(w2_all[:].bitcast(I32), w2_words[0].rearrange("p m d -> p (m d)").bitcast(I32))
+        load_words(w2_all, w2_words[0])
 
         w1s_listed = keep.tile([P, G * H], U8, name="w1s_listed", align_bytes=ALIGN)
         w1s = keep.tile([P, G, PACK, P], U8, name="w1s", align_bytes=ALIGN)
@@ -118,83 +122,99 @@ def tile_moe_wsel_b_relu_p_kernel(
             entries = slice(r * H // PER_COLUMN, (r + 1) * H // PER_COLUMN)
             nc.vector.tensor_copy(w1[s][r][:].rearrange("p d m -> p m d"), w1_all[s][:].indirect(list1[:, entries]))
 
-        def turned_pass(j, r, s):
-            nc.tensor.matmul_mx(
-                turned_sum[j, r][:],
-                lhsT=x_turned[:, s, j * TT : (j + 1) * TT].bitcast(FP8X4),
-                lhsT_scale=xs[:, s, j * TT : (j + 1) * TT],
-                rhs=w1[s][r][:].rearrange("p d m -> p (d m)").bitcast(FP8X4),
-                rhs_scale=w1s[W1_ROWS * s :, r].rearrange("p d m -> p (d m)"),
-                start=(s == 0),
-                stop=(s == PASSES - 1),
-            )
+        sums = {}
+        turned_units = [(0, 0), (1, 0), (0, 1), (1, 1), (2, 1)]
+
+        def first_pass(j, r, s):
+            tokens = slice(j * TT, (j + 1) * TT)
+            if s == 0:
+                sums[j, r] = psum.tile([P, PACK, TT], F32, name="sums", tag="bank")
+            if (j, r) in turned_units:
+                nc.tensor.matmul_mx(
+                    sums[j, r][:].rearrange("t d m -> t (d m)"),
+                    lhsT=x[j // 2][:, s, (j % 2) * TT : (j % 2 + 1) * TT].bitcast(FP8X4),
+                    lhsT_scale=xs[:, s, tokens],
+                    rhs=w1[s][r][:].rearrange("p d m -> p (d m)").bitcast(FP8X4),
+                    rhs_scale=w1s[W1_ROWS * s :, r].rearrange("p d m -> p (d m)"),
+                    start=(s == 0),
+                    stop=(s == PASSES - 1),
+                )
+            else:
+                for d in range(PACK):
+                    nc.tensor.matmul_mx(
+                        sums[j, r][:, d, :],
+                        lhsT=w1[s][r][:, d, :].bitcast(FP8X4),
+                        lhsT_scale=w1s[W1_ROWS * s :, r, d, :],
+                        rhs=x[1][:, s, j * TT - HALF : (j + 1) * TT - HALF].bitcast(FP8X4),
+                        rhs_scale=xs[:, s, tokens],
+                        start=(s == 0 and d == 0),
+                        stop=(s == PASSES - 1 and d == PACK - 1),
+                    )
 
         gate_turned = psum.tile([P, P], F32, name="gate_turned", tag="bank")
         nc.tensor.transpose(gate_turned[:], gate_few[:], ident[:])
-        gate_cols = keep.tile([P, G, TURNED], F32, name="gate_cols")
-        nc.scalar.copy(gate_cols[:].rearrange("t r j -> t (r j)"), gate_turned[:, 0 : G * TURNED])
+        gate_size = keep.tile([P, G * TURNED], F32, name="gate_size")
+        gate_sign = keep.tile([P, G * TURNED], F32, name="gate_sign")
+        nc.scalar.activation(gate_size[:], gate_turned[:, 0 : G * TURNED], ABS)
+        nc.scalar.activation(gate_sign[:], gate_turned[:, 0 : G * TURNED], SIGN)
 
-        turned_sum = {}
         for r in range(G):
             gather_w1(0, r)
-            for j in range(TURNED):
-                turned_sum[j, r] = psum.tile([P, H], F32, name="turned_sum", tag="bank")
-                turned_pass(j, r, 0)
+            for j in range(2):
+                first_pass(j, r, 0)
         for r in range(G):
             gather_w1(1, r)
-        w2s = stage.tile([P, G * N], U8, name="w2s", align_bytes=ALIGN, offset=w1_at[1])
-        nc.vector.tensor_copy(w2s[:], w2s_all[:].indirect(list2[:]))
 
-        h_turned = [keep.tile([P, G, H], BF16, name="h_turned%d" % j, align_bytes=ALIGN) for j in range(TURNED)]
+        def both_passes(j, r):
+            for s in range(PASSES):
+                first_pass(j, r, s)
+
+        h_turned, backs = {}, {}
         h, hq, hs = {}, {}, {}
-        for j in range(T // TT):
+        for j in range(TILES):
+            h[j] = keep.tile([P, G, TT * PACK], BF16, name="h%d" % j, align_bytes=ALIGN)
             hq[j] = keep.tile([P, G, TT], U32, name="hq%d" % j, align_bytes=ALIGN)
             hs[j] = keep.tile([P, G, TT], U8, name="hs%d" % j, align_bytes=ALIGN)
 
-        def turned(j, r, gate_on_vector):
-            turned_pass(j, r, PASSES - 1)
-            relu = keep.tile([P, 2, P, 2], F32, name="relu", tag="relu%d%d" % (j, r), align_bytes=ALIGN)
-            nc.scalar.activation(relu[:], turned_sum[j, r][:].rearrange("t (u e m) -> t u m e", u=2, e=2), RELU)
-            relu_flat = relu[:].rearrange("t u m e -> t (u m e)")
-            gate_col = gate_cols[:, r, j : j + 1]
-            if gate_on_vector:
-                nc.vector.tensor_scalar(h_turned[j][:, r, :], relu_flat, gate_col, None, MULT)
+        def turned(j, r):
+            h_turned[j, r] = keep.tile([P, 2, P, 2], BF16, name="h_turned%d%d" % (j, r), align_bytes=ALIGN)
+            src = sums[j, r][:].rearrange("t (u e) m -> t u m e", u=2)
+            col = slice(r * TURNED + j, r * TURNED + j + 1)
+            nc.scalar.activation(h_turned[j, r][:], src, RELU, scale=gate_size[:, col])
+
+        def sign(j, r, on_vector):
+            col = slice(r * TURNED + j, r * TURNED + j + 1)
+            flat = h_turned[j, r][:].rearrange("t u m e -> t (u m e)")
+            if on_vector:
+                nc.vector.tensor_scalar(flat, flat, gate_sign[:, col], None, MULT)
             else:
-                nc.scalar.activation(h_turned[j][:, r, :], relu_flat, COPY, scale=gate_col)
+                nc.gpsimd.tensor_scalar(flat, flat, gate_sign[:, col], 0.0, MULT, ADD)
 
-        def turn_back(j):
-            back = psum.tile([P, G, 2, TT], F32, name="back", tag="bank")
-            for r in range(G):
+        def turn(j):
+            experts = [r for r in range(G) if (j, r) in turned_units]
+            backs[j] = psum.tile([P, len(experts), 2, TT], F32, name="back", tag="bank")
+            for n, r in enumerate(experts):
                 for u in range(2):
-                    pairs = h_turned[j][:, r, :].bitcast(F32)[:, u * P : (u + 1) * P]
-                    nc.tensor.transpose(back[:, r, u, :], pairs, ident[:])
-            h[j] = keep.tile([P, G, TT * PACK], BF16, name="h%d" % j, align_bytes=ALIGN)
-            nc.scalar.copy(h[j][:].bitcast(F32).rearrange("p r (t u) -> p r t u", u=2), back[:].rearrange("p r u t -> p r t u"))
+                    pairs = h_turned[j, r][:].rearrange("t u m e -> t (u m e)").bitcast(F32)[:, u * P : (u + 1) * P]
+                    nc.tensor.transpose(backs[j][:, n, u, :], pairs, ident[:])
 
-        def direct(j, r, dst):
+        def copy_back(j):
+            experts = [r for r in range(G) if (j, r) in turned_units]
+            dst = h[j][:, experts[0] : experts[-1] + 1, :].bitcast(F32).rearrange("p r (t u) -> p r t u", u=2)
+            nc.scalar.copy(dst, backs[j][:].rearrange("p r u t -> p r t u"))
+
+        def direct(j, r):
             tokens = slice(j * TT - HALF, (j + 1) * TT - HALF)
-            direct_sum = psum.tile([P, PACK, TT], F32, name="direct_sum", tag="bank")
-            for d in range(PACK):
-                for s in range(PASSES):
-                    nc.tensor.matmul_mx(
-                        direct_sum[:, d, :],
-                        lhsT=w1[s][r][:, d, :].bitcast(FP8X4),
-                        lhsT_scale=w1s[W1_ROWS * s :, r, d, :],
-                        rhs=x_direct[:, s, tokens].bitcast(FP8X4),
-                        rhs_scale=xs[:, s, j * TT : (j + 1) * TT],
-                        start=(s == 0),
-                        stop=(s == PASSES - 1),
-                    )
             nc.vector.scalar_tensor_tensor(
-                dst.rearrange("p (t d) -> p t d", d=PACK),
-                direct_sum[:].rearrange("p d t -> p t d"),
+                h[j][:, r, :].rearrange("p (t d) -> p t d", d=PACK),
+                sums[j, r][:].rearrange("p d t -> p t d"),
                 0.0,
                 gate_rows[:, r, tokens].unsqueeze(2).to_broadcast([P, TT, PACK]),
                 MAX,
                 MULT,
             )
 
-        def quantise_both(j):
+        def quantise(j):
             nc.vector.quantize_mx(
                 hq[j][:].rearrange("p r t -> p (r t)").bitcast(FP8X4),
                 hs[j][:].rearrange("p r t -> p (r t)"),
@@ -203,56 +223,60 @@ def tile_moe_wsel_b_relu_p_kernel(
 
         out_hbm = out.rearrange("(c p) t -> p c t", p=P)
 
-        def second_pass(dst, c, r, j):
-            cols = slice(r * N + c * P, r * N + (c + 1) * P)
-            nc.tensor.matmul_mx(
-                dst,
-                lhsT=w2[:, cols].bitcast(FP8X4),
-                lhsT_scale=w2s[W2_ROW:, cols],
-                rhs=hq[j][:, r, :].bitcast(FP8X4),
-                rhs_scale=hs[j][:, r, :],
-                start=(r == 0),
-                stop=(r == G - 1),
-            )
-
-        def second_layer(j, queue):
+        def second_layer(j, on_vector):
             out_sum = psum.tile([P, OUT_TILES, TT], F32, name="out_sum", tag="bank")
             for c in range(OUT_TILES):
                 for r in range(G):
-                    second_pass(out_sum[:, c, :], c, r, j)
+                    cols = slice(r * N + c * P, r * N + (c + 1) * P)
+                    nc.tensor.matmul_mx(
+                        out_sum[:, c, :],
+                        lhsT=w2[:, cols].bitcast(FP8X4),
+                        lhsT_scale=w2s[W2_ROW:, cols],
+                        rhs=hq[j][:, r, :].bitcast(FP8X4),
+                        rhs_scale=hs[j][:, r, :],
+                        start=(r == 0),
+                        stop=(r == G - 1),
+                    )
             result = keep.tile([P, OUT_TILES, TT], F32, name="result%d" % j)
-            nc.scalar.copy(result[:], out_sum[:])
-            queue.dma_start(out_hbm[:, :, j * TT : (j + 1) * TT], result[:])
+            if on_vector:
+                nc.vector.tensor_copy(result[:], out_sum[:])
+            else:
+                nc.scalar.copy(result[:], out_sum[:])
+            nc.sync.dma_start(out_hbm[:, :, j * TT : (j + 1) * TT], result[:])
 
-        h[2] = keep.tile([P, G, TT * PACK], BF16, name="h2", align_bytes=ALIGN)
-        turned(0, 0, gate_on_vector=True)
-        turned(1, 0, gate_on_vector=False)
-        direct(2, 0, h[2][:, 0, :])
-        w2 = keep.tile([P, G * N], U32, name="w2", tag="relu10", align_bytes=ALIGN)
+        w2s = stage.tile([P, G * N], U8, name="w2s", align_bytes=ALIGN, offset=w1_at[1])
+        nc.vector.tensor_copy(w2s[:], w2s_all[:].indirect(list2[:]))
+        first_pass(0, 0, 1)
+        first_pass(1, 0, 1)
+        both_passes(2, 0)
+        first_pass(0, 1, 1)
+        first_pass(1, 1, 1)
+        both_passes(2, 1)
+        both_passes(3, 0)
+        for j, r in turned_units:
+            turned(j, r)
+        sign(0, 0, False)
+        sign(1, 0, False)
+        sign(1, 1, False)
+        direct(2, 0)
+        w2 = keep.tile([P, G * N], U32, name="w2", tag="w1_0_0", align_bytes=ALIGN)
         nc.vector.tensor_copy(w2[:], w2_all[:].indirect(list2[:]))
-        turned(0, 1, gate_on_vector=True)
-        turned(1, 1, gate_on_vector=False)
-        direct(2, 1, h[2][:, 1, :])
-        turn_back(0)
-        h3_first = stage.tile([P, TT * PACK], BF16, name="h3_first", align_bytes=ALIGN, offset=w2_at)
-        direct(3, 0, h3_first[:])
-        turn_back(1)
-        quantise_both(2)
-        h3_second = keep.tile([P, TT * PACK], BF16, name="h3_second", align_bytes=ALIGN)
-        direct(3, 1, h3_second[:])
-        quantise_both(0)
-        second_layer(2, nc.sync)
-        second_layer(0, nc.sync)
-
-        last_sum = [psum.tile([P, TT], F32, name="last_sum%d" % c, tag="bank") for c in range(OUT_TILES)]
-        nc.vector.quantize_mx(hq[3][:, 0, :].bitcast(FP8X4), hs[3][:, 0, :], h3_first[:])
-        for c in range(OUT_TILES):
-            second_pass(last_sum[c][:], c, 0, 3)
-        quantise_both(1)
-        second_layer(1, nc.scalar)
-        nc.vector.quantize_mx(hq[3][:, 1, :].bitcast(FP8X4), hs[3][:, 1, :], h3_second[:])
-        last_result = keep.tile([P, OUT_TILES, TT], F32, name="last_result")
-        for c in range(OUT_TILES):
-            second_pass(last_sum[c][:], c, 1, 3)
-            nc.vector.tensor_copy(last_result[:, c, :], last_sum[c][:])
-        nc.sync.dma_start(out_hbm[:, :, 3 * TT : 4 * TT], last_result[:])
+        sign(0, 1, True)
+        turn(0)
+        both_passes(3, 1)
+        direct(3, 0)
+        sign(2, 1, True)
+        turn(1)
+        turn(2)
+        copy_back(0)
+        copy_back(1)
+        copy_back(2)
+        quantise(0)
+        direct(3, 1)
+        second_layer(0, False)
+        quantise(1)
+        quantise(3)
+        second_layer(1, False)
+        quantise(2)
+        second_layer(3, False)
+        second_layer(2, True)

@@ -17,6 +17,7 @@ MAX = mybir.AluOpType.max
 MULT = mybir.AluOpType.mult
 ADD = mybir.AluOpType.add
 RELU = mybir.ActivationFunctionType.Relu
+COPY = mybir.ActivationFunctionType.Copy
 ABS = mybir.ActivationFunctionType.Abs
 SIGN = mybir.ActivationFunctionType.Sign
 
@@ -28,7 +29,6 @@ PER_COLUMN = 16
 TT = 128
 TILES = T // TT
 HALF = T // 2
-TURNED = 3
 OUT_TILES = N // P
 W1_ROWS = 4
 W2_ROW = 8
@@ -42,7 +42,7 @@ def tile_moe_wsel_b_relu_p_kernel(
     with ExitStack() as ctx:
         keep = ctx.enter_context(tc.tile_pool(name="keep", bufs=1))
         stage = ctx.enter_context(tc.tile_pool(name="stage", bufs=1))
-        psum = ctx.enter_context(tc.psum_pool(name="psum", bufs=8))
+        psum = ctx.enter_context(tc.psum_pool(name="psum", bufs=1))
 
         list1 = keep.tile([P, G * H // PER_COLUMN], U16, name="list1")
         list2 = keep.tile([P, G * N // PER_COLUMN], U16, name="list2")
@@ -50,9 +50,12 @@ def tile_moe_wsel_b_relu_p_kernel(
         w2s_all = keep.tile([P, E * N], U8, name="w2s_all", align_bytes=ALIGN)
         xs = keep.tile([P, PASSES, T], U8, name="xs", align_bytes=ALIGN)
         ident = keep.tile([P, P], F32, name="ident")
+        gate_few = keep.tile([P, TT], F32, name="gate_few")
+        nc.gpsimd.memset(gate_few[:], 0.0)
+        nc.gpsimd.dma_start(gate_few[0:TILES, :], gate[0, 0, :].rearrange("(j t) -> j t", t=TT))
         make_identity(nc, ident[:])
 
-        stage_words = PASSES * E * H + E * N + PASSES * HALF + G * HALF + TT
+        stage_words = PASSES * E * H + E * N + T + T
         xs_words = PASSES * T // 4
         zeros = stage.tile([P, stage_words], I32, name="zeros", offset=0, align_bytes=ALIGN)
         nc.vector.memset(w1s_all[:].bitcast(I32), 0)
@@ -63,111 +66,131 @@ def tile_moe_wsel_b_relu_p_kernel(
         w1_at = [4 * E * H * s for s in range(PASSES)]
         w2_at = 4 * E * H * PASSES
         x_at = w2_at + 4 * E * N
-        gate_rows_at = x_at + 4 * PASSES * HALF
-        gate_few_at = gate_rows_at + 4 * G * HALF
+        gate_rows_at = x_at + 4 * T
         w1_all = [
             stage.tile([P, E * H], U32, name="w1_all%d" % s, align_bytes=ALIGN, offset=w1_at[s]) for s in range(PASSES)
         ]
         w2_all = stage.tile([P, E * N], U32, name="w2_all", align_bytes=ALIGN, offset=w2_at)
         x = [
-            keep.tile([P, PASSES, HALF], U32, name="x0", align_bytes=ALIGN),
-            stage.tile([P, PASSES, HALF], U32, name="x1", align_bytes=ALIGN, offset=x_at),
+            keep.tile([P, T], U32, name="x0", align_bytes=ALIGN),
+            stage.tile([P, T], U32, name="x1", align_bytes=ALIGN, offset=x_at),
         ]
-        gate_rows = stage.tile([P, G, HALF], F32, name="gate_rows", align_bytes=ALIGN, offset=gate_rows_at)
-        gate_few = stage.tile([P, TT], F32, name="gate_few", align_bytes=ALIGN, offset=gate_few_at)
-        nc.gpsimd.memset(gate_few[:], 0.0)
+        gate_rows = stage.tile([P, T], F32, name="gate_rows", align_bytes=ALIGN, offset=gate_rows_at)
 
         def load_words(dst, src):
             nc.sync.dma_start(dst[:].bitcast(I32), src.rearrange("p m d -> p (m d)").bitcast(I32))
 
-        x_hbm = x_words.rearrange("s p t d -> p s (t d)").bitcast(I32)
-        nc.sync.dma_start(list1[:], offs)
-        nc.sync.dma_start(x[0][:].bitcast(I32), x_hbm[:, :, 0:HALF])
-        nc.sync.dma_start(list2[:], offs2)
-        for q in range(QUADRANTS):
+        def load_w1_scales(q):
             nc.sync.dma_start(
                 w1s_all[:].bitcast(I32)[32 * q : 32 * q + W1_ROWS * PASSES, :],
                 w1_scales.bitcast(I32)[:, 4 * q : 4 * q + 4, :],
             )
-        load_words(w1_all[0], w1_words[0])
-        for q in range(QUADRANTS):
+
+        def load_x_scales(q):
             nc.sync.dma_start(
                 xs[:].bitcast(I32)[32 * q : 32 * q + 4],
                 x_scales.bitcast(I32)[:, 4 * q : 4 * q + 4, :].rearrange("s j t -> j s t"),
             )
-        nc.sync.dma_start(gate_few[0 : G * TURNED, :], gate[:, 0, 0 : TURNED * TT].rearrange("r (j t) -> r j t", t=TT))
-        load_words(w1_all[1], w1_words[1])
-        nc.sync.dma_start(x[1][:].bitcast(I32), x_hbm[:, :, HALF:T])
-        nc.sync.dma_start(gate_rows[:], gate.rearrange("r p t -> p r t")[:, :, HALF:T])
-        for q in range(QUADRANTS):
+
+        def load_w2_scales(q):
             nc.sync.dma_start(
                 w2s_all[:].bitcast(I32)[32 * q + W2_ROW : 32 * q + W2_ROW + 4, :],
                 w2_scales.bitcast(I32)[0, 4 * q : 4 * q + 4, :],
             )
+
+        nc.sync.dma_start(list1[:], offs)
+        load_words(x[0], x_words[0])
+        nc.sync.dma_start(list2[:], offs2)
+        for q in range(QUADRANTS):
+            load_w1_scales(q)
+        load_words(w1_all[0], w1_words[0])
+        for q in range(QUADRANTS):
+            load_x_scales(q)
+        load_words(w1_all[1], w1_words[1])
+        load_words(x[1], x_words[1])
+        for q in range(QUADRANTS):
+            load_w2_scales(q)
+        nc.sync.dma_start(gate_rows[:], gate[1])
         load_words(w2_all, w2_words[0])
 
-        w1s_listed = keep.tile([P, G * H], U8, name="w1s_listed", align_bytes=ALIGN)
-        w1s = keep.tile([P, G, PACK, P], U8, name="w1s", align_bytes=ALIGN)
+        w1s = keep.tile([P, G * H], U8, name="w1s", align_bytes=ALIGN)
+        w1s_dm = keep.tile([P, PACK, P], U8, name="w1s_dm", align_bytes=ALIGN)
         w1 = [
-            [keep.tile([P, PACK, P], U32, name="w1_%d_%d" % (s, r), align_bytes=ALIGN) for r in range(G)]
+            [keep.tile([P, H], U32, name="w1_%d_%d" % (s, r), align_bytes=ALIGN) for r in range(G)]
             for s in range(PASSES)
         ]
-        nc.vector.tensor_copy(w1s_listed[:], w1s_all[:].indirect(list1[:]))
-        nc.vector.tensor_copy(
-            w1s[:].rearrange("p r d (a m) -> p r a d m", m=16),
-            w1s_listed[:].rearrange("p (r a m d) -> p r a d m", r=G, m=16, d=PACK),
-        )
+        for r in range(G):
+            entries = slice(r * H // PER_COLUMN, (r + 1) * H // PER_COLUMN)
+            nc.vector.tensor_copy(w1s[:, r * H : (r + 1) * H], w1s_all[:].indirect(list1[:, entries]))
+        warm = psum.tile([P, T], F32, name="warm", tag="bank7")
+        for i in range(4):
+            nc.tensor.matmul_mx(
+                warm[:],
+                lhsT=x[0][:, 0:P].bitcast(FP8X4),
+                lhsT_scale=w1s[:, 0:P],
+                rhs=x[0][:].bitcast(FP8X4),
+                rhs_scale=w1s[:, 0:T],
+                start=True,
+                stop=True,
+            )
+
+        def permute_scales():
+            nc.vector.tensor_copy(
+                w1s_dm[:].rearrange("p d (a m) -> p a d m", m=16),
+                w1s[:, H : 2 * H].rearrange("p (a m d) -> p a d m", m=16, d=PACK),
+            )
 
         def gather_w1(s, r):
             entries = slice(r * H // PER_COLUMN, (r + 1) * H // PER_COLUMN)
-            nc.vector.tensor_copy(w1[s][r][:].rearrange("p d m -> p m d"), w1_all[s][:].indirect(list1[:, entries]))
+            dst = w1[s][r][:].rearrange("p (m d) -> p m d", d=PACK)
+            if r == 1:
+                dst = w1[s][r][:].rearrange("p (d m) -> p m d", d=PACK)
+            nc.vector.tensor_copy(dst, w1_all[s][:].indirect(list1[:, entries]))
 
         sums = {}
-        turned_units = [(0, 0), (1, 0), (0, 1), (1, 1), (2, 1)]
+        sum_bank = {(0, 0): 0, (1, 0): 1, (2, 0): 2, (3, 0): 3, (0, 1): 4, (1, 1): 5, (2, 1): 7, (3, 1): 6}
+        back_bank = [0, 1, 2, 3]
+        out_bank = [4, 5, 0]
 
         def first_pass(j, r, s):
             tokens = slice(j * TT, (j + 1) * TT)
+            words = x[s][:, tokens].bitcast(FP8X4)
             if s == 0:
-                sums[j, r] = psum.tile([P, PACK, TT], F32, name="sums", tag="bank")
-            if (j, r) in turned_units:
+                sums[j, r] = psum.tile([P, H], F32, name="sums", tag="bank%d" % sum_bank[j, r])
+            if r == 0:
                 nc.tensor.matmul_mx(
-                    sums[j, r][:].rearrange("t d m -> t (d m)"),
-                    lhsT=x[j // 2][:, s, (j % 2) * TT : (j % 2 + 1) * TT].bitcast(FP8X4),
+                    sums[j, r][:],
+                    lhsT=words,
                     lhsT_scale=xs[:, s, tokens],
-                    rhs=w1[s][r][:].rearrange("p d m -> p (d m)").bitcast(FP8X4),
-                    rhs_scale=w1s[W1_ROWS * s :, r].rearrange("p d m -> p (d m)"),
+                    rhs=w1[s][r][:].bitcast(FP8X4),
+                    rhs_scale=w1s[W1_ROWS * s :, 0:H],
                     start=(s == 0),
                     stop=(s == PASSES - 1),
                 )
             else:
                 for d in range(PACK):
                     nc.tensor.matmul_mx(
-                        sums[j, r][:, d, :],
-                        lhsT=w1[s][r][:, d, :].bitcast(FP8X4),
-                        lhsT_scale=w1s[W1_ROWS * s :, r, d, :],
-                        rhs=x[1][:, s, j * TT - HALF : (j + 1) * TT - HALF].bitcast(FP8X4),
+                        sums[j, r][:, d * TT : (d + 1) * TT],
+                        lhsT=w1[s][r][:, d * P : (d + 1) * P].bitcast(FP8X4),
+                        lhsT_scale=w1s_dm[W1_ROWS * s :, d, :],
+                        rhs=words,
                         rhs_scale=xs[:, s, tokens],
                         start=(s == 0 and d == 0),
                         stop=(s == PASSES - 1 and d == PACK - 1),
                     )
 
-        gate_turned = psum.tile([P, P], F32, name="gate_turned", tag="bank")
-        nc.tensor.transpose(gate_turned[:], gate_few[:], ident[:])
-        gate_size = keep.tile([P, G * TURNED], F32, name="gate_size")
-        gate_sign = keep.tile([P, G * TURNED], F32, name="gate_sign")
-        nc.scalar.activation(gate_size[:], gate_turned[:, 0 : G * TURNED], ABS)
-        nc.scalar.activation(gate_sign[:], gate_turned[:, 0 : G * TURNED], SIGN)
-
-        for r in range(G):
-            gather_w1(0, r)
-            for j in range(2):
-                first_pass(j, r, 0)
-        for r in range(G):
-            gather_w1(1, r)
-
         def both_passes(j, r):
             for s in range(PASSES):
                 first_pass(j, r, s)
+
+        gate_size = keep.tile([P, TILES], F32, name="gate_size")
+        gate_sign = keep.tile([P, TILES], F32, name="gate_sign")
+
+        def gate_columns():
+            gate_turned = psum.tile([P, P], F32, name="gate_turned", tag="bank6")
+            nc.tensor.transpose(gate_turned[:], gate_few[:], ident[:])
+            nc.scalar.activation(gate_size[:], gate_turned[:, 0:TILES], ABS)
+            nc.scalar.activation(gate_sign[:], gate_turned[:, 0:TILES], SIGN)
 
         h_turned, backs = {}, {}
         h, hq, hs = {}, {}, {}
@@ -176,40 +199,40 @@ def tile_moe_wsel_b_relu_p_kernel(
             hq[j] = keep.tile([P, G, TT], U32, name="hq%d" % j, align_bytes=ALIGN)
             hs[j] = keep.tile([P, G, TT], U8, name="hs%d" % j, align_bytes=ALIGN)
 
-        def turned(j, r):
-            h_turned[j, r] = keep.tile([P, 2, P, 2], BF16, name="h_turned%d%d" % (j, r), align_bytes=ALIGN)
-            src = sums[j, r][:].rearrange("t (u e) m -> t u m e", u=2)
-            col = slice(r * TURNED + j, r * TURNED + j + 1)
-            nc.scalar.activation(h_turned[j, r][:], src, RELU, scale=gate_size[:, col])
+        def turned(j):
+            h_turned[j] = keep.tile([P, H], BF16, name="h_turned%d" % j, align_bytes=ALIGN)
+            nc.scalar.activation(
+                h_turned[j][:].rearrange("t (u m e) -> t u m e", u=2, e=2),
+                sums[j, 0][:].rearrange("t (m u e) -> t u m e", u=2, e=2),
+                RELU,
+                scale=gate_size[:, j : j + 1],
+            )
 
-        def sign(j, r, on_vector):
-            col = slice(r * TURNED + j, r * TURNED + j + 1)
-            flat = h_turned[j, r][:].rearrange("t u m e -> t (u m e)")
-            if on_vector:
-                nc.vector.tensor_scalar(flat, flat, gate_sign[:, col], None, MULT)
+        def sign(j, engine):
+            flat = h_turned[j][:]
+            if engine == "vector":
+                nc.vector.tensor_scalar(flat, flat, gate_sign[:, j : j + 1], None, MULT)
+            elif engine == "scalar":
+                nc.scalar.activation(flat, flat, COPY, scale=gate_sign[:, j : j + 1])
             else:
-                nc.gpsimd.tensor_scalar(flat, flat, gate_sign[:, col], 0.0, MULT, ADD)
+                nc.gpsimd.tensor_scalar(flat, flat, gate_sign[:, j : j + 1], 0.0, MULT, ADD)
 
         def turn(j):
-            experts = [r for r in range(G) if (j, r) in turned_units]
-            backs[j] = psum.tile([P, len(experts), 2, TT], F32, name="back", tag="bank")
-            for n, r in enumerate(experts):
-                for u in range(2):
-                    pairs = h_turned[j, r][:].rearrange("t u m e -> t (u m e)").bitcast(F32)[:, u * P : (u + 1) * P]
-                    nc.tensor.transpose(backs[j][:, n, u, :], pairs, ident[:])
+            backs[j] = psum.tile([P, 2, TT], F32, name="back", tag="bank%d" % back_bank[j])
+            for u in range(2):
+                nc.tensor.transpose(backs[j][:, u, :], h_turned[j][:].bitcast(F32)[:, u * P : (u + 1) * P], ident[:])
 
         def copy_back(j):
-            experts = [r for r in range(G) if (j, r) in turned_units]
-            dst = h[j][:, experts[0] : experts[-1] + 1, :].bitcast(F32).rearrange("p r (t u) -> p r t u", u=2)
-            nc.scalar.copy(dst, backs[j][:].rearrange("p r u t -> p r t u"))
+            nc.scalar.copy(
+                h[j][:, 0, :].bitcast(F32).rearrange("p (t u) -> p t u", u=2), backs[j][:].rearrange("p u t -> p t u")
+            )
 
-        def direct(j, r):
-            tokens = slice(j * TT - HALF, (j + 1) * TT - HALF)
+        def direct(j):
             nc.vector.scalar_tensor_tensor(
-                h[j][:, r, :].rearrange("p (t d) -> p t d", d=PACK),
-                sums[j, r][:].rearrange("p d t -> p t d"),
+                h[j][:, 1, :].rearrange("p (t d) -> p t d", d=PACK),
+                sums[j, 1][:].rearrange("p (d t) -> p t d", d=PACK),
                 0.0,
-                gate_rows[:, r, tokens].unsqueeze(2).to_broadcast([P, TT, PACK]),
+                gate_rows[:, j * TT : (j + 1) * TT].unsqueeze(2).to_broadcast([P, TT, PACK]),
                 MAX,
                 MULT,
             )
@@ -221,22 +244,28 @@ def tile_moe_wsel_b_relu_p_kernel(
                 h[j][:].rearrange("p r c -> p (r c)"),
             )
 
+        def quantise_one(j, r):
+            nc.vector.quantize_mx(hq[j][:, r, :].bitcast(FP8X4), hs[j][:, r, :], h[j][:, r, :])
+
         out_hbm = out.rearrange("(c p) t -> p c t", p=P)
 
+        def second_pass(dst, c, r, j):
+            cols = slice(r * N + c * P, r * N + (c + 1) * P)
+            nc.tensor.matmul_mx(
+                dst,
+                lhsT=w2[:, cols].bitcast(FP8X4),
+                lhsT_scale=w2s[W2_ROW:, cols],
+                rhs=hq[j][:, r, :].bitcast(FP8X4),
+                rhs_scale=hs[j][:, r, :],
+                start=(r == 0),
+                stop=(r == G - 1),
+            )
+
         def second_layer(j, on_vector):
-            out_sum = psum.tile([P, OUT_TILES, TT], F32, name="out_sum", tag="bank")
+            out_sum = psum.tile([P, OUT_TILES, TT], F32, name="out_sum", tag="bank%d" % out_bank[j])
             for c in range(OUT_TILES):
                 for r in range(G):
-                    cols = slice(r * N + c * P, r * N + (c + 1) * P)
-                    nc.tensor.matmul_mx(
-                        out_sum[:, c, :],
-                        lhsT=w2[:, cols].bitcast(FP8X4),
-                        lhsT_scale=w2s[W2_ROW:, cols],
-                        rhs=hq[j][:, r, :].bitcast(FP8X4),
-                        rhs_scale=hs[j][:, r, :],
-                        start=(r == 0),
-                        stop=(r == G - 1),
-                    )
+                    second_pass(out_sum[:, c, :], c, r, j)
             result = keep.tile([P, OUT_TILES, TT], F32, name="result%d" % j)
             if on_vector:
                 nc.vector.tensor_copy(result[:], out_sum[:])
@@ -244,39 +273,54 @@ def tile_moe_wsel_b_relu_p_kernel(
                 nc.scalar.copy(result[:], out_sum[:])
             nc.sync.dma_start(out_hbm[:, :, j * TT : (j + 1) * TT], result[:])
 
+        gate_columns()
+        permute_scales()
+        gather_w1(0, 0)
+        for j in range(TILES):
+            first_pass(j, 0, 0)
+        gather_w1(0, 1)
+        for j in range(TILES):
+            first_pass(j, 1, 0)
+        for r in range(G):
+            gather_w1(1, r)
         w2s = stage.tile([P, G * N], U8, name="w2s", align_bytes=ALIGN, offset=w1_at[1])
         nc.vector.tensor_copy(w2s[:], w2s_all[:].indirect(list2[:]))
-        first_pass(0, 0, 1)
-        first_pass(1, 0, 1)
-        both_passes(2, 0)
-        first_pass(0, 1, 1)
-        first_pass(1, 1, 1)
-        both_passes(2, 1)
-        both_passes(3, 0)
-        for j, r in turned_units:
-            turned(j, r)
-        sign(0, 0, False)
-        sign(1, 0, False)
-        sign(1, 1, False)
-        direct(2, 0)
-        w2 = keep.tile([P, G * N], U32, name="w2", tag="w1_0_0", align_bytes=ALIGN)
+        for j in range(TILES):
+            first_pass(j, 0, 1)
+        for j in range(TILES):
+            first_pass(j, 1, 1)
+        for j in range(TILES):
+            turned(j)
+        for j in range(3):
+            sign(j, "gpsimd")
+        sign(3, "scalar")
+        direct(0)
+        direct(1)
+        w2 = keep.tile([P, G * N], U32, name="w2", tag="w1_1_0", align_bytes=ALIGN)
         nc.vector.tensor_copy(w2[:], w2_all[:].indirect(list2[:]))
-        sign(0, 1, True)
         turn(0)
-        both_passes(3, 1)
-        direct(3, 0)
-        sign(2, 1, True)
         turn(1)
+        turn(3)
         turn(2)
-        copy_back(0)
-        copy_back(1)
-        copy_back(2)
+        for j in (0, 1, 3, 2):
+            copy_back(j)
+        direct(2)
         quantise(0)
-        direct(3, 1)
         second_layer(0, False)
         quantise(1)
-        quantise(3)
+        direct(3)
         second_layer(1, False)
+        quantise_one(3, 0)
         quantise(2)
-        second_layer(3, False)
-        second_layer(2, True)
+        second_layer(2, False)
+        last_sum = [psum.tile([P, TT], F32, name="last_sum%d" % c, tag="bank%d" % (1 + 2 * c)) for c in range(OUT_TILES)]
+        for c in range(OUT_TILES):
+            second_pass(last_sum[c][:], c, 0, 3)
+        quantise_one(3, 1)
+        last = [keep.tile([P, TT], F32, name="last%d" % c) for c in range(OUT_TILES)]
+        for c in range(OUT_TILES):
+            second_pass(last_sum[c][:], c, 1, 3)
+        nc.vector.tensor_copy(last[0][:], last_sum[0][:])
+        nc.sync.dma_start(out_hbm[:, 0, 3 * TT : 4 * TT], last[0][:])
+        nc.scalar.copy(last[1][:], last_sum[1][:])
+        nc.scalar.dma_start(out_hbm[:, 1, 3 * TT : 4 * TT], last[1][:])

@@ -148,8 +148,8 @@ def tile_moe_wsel_b_relu_p_kernel(
             nc.vector.tensor_copy(dst, w1_all[s][:].indirect(list1[:, entries]))
 
         sums = {}
-        sum_bank = {(0, 0): 0, (1, 0): 1, (2, 0): 2, (3, 0): 3, (0, 1): 4, (1, 1): 5, (2, 1): 7, (3, 1): 6}
-        back_bank = [0, 1, 2, 3]
+        sum_bank = {(0, 0): 0, (1, 0): 1, (2, 0): 2, (3, 0): 3, (0, 1): 4, (1, 1): 5, (2, 1): 7, (3, 1): 3}
+        back_bank = [0, 1, 2, 6]
         out_bank = [4, 5, 0]
 
         def first_pass(j, r, s):
@@ -279,7 +279,7 @@ def tile_moe_wsel_b_relu_p_kernel(
         for j in range(TILES):
             first_pass(j, 0, 0)
         gather_w1(0, 1)
-        for j in range(TILES):
+        for j in range(TILES - 1):
             first_pass(j, 1, 0)
         for r in range(G):
             gather_w1(1, r)
@@ -287,10 +287,11 @@ def tile_moe_wsel_b_relu_p_kernel(
         nc.vector.tensor_copy(w2s[:], w2s_all[:].indirect(list2[:]))
         for j in range(TILES):
             first_pass(j, 0, 1)
-        for j in range(TILES):
+        for j in range(TILES - 1):
             first_pass(j, 1, 1)
         for j in range(TILES):
             turned(j)
+        both_passes(TILES - 1, 1)
         for j in range(3):
             sign(j, "gpsimd")
         sign(3, "scalar")

@@ -51,8 +51,6 @@ def tile_moe_wsel_b_relu_p_kernel(
         xs = keep.tile([P, PASSES, T], U8, name="xs", align_bytes=ALIGN)
         ident = keep.tile([P, P], F32, name="ident")
         gate_few = keep.tile([P, TT], F32, name="gate_few")
-        nc.gpsimd.memset(gate_few[:], 0.0)
-        nc.gpsimd.dma_start(gate_few[0:TILES, :], gate[0, 0, :].rearrange("(j t) -> j t", t=TT))
         make_identity(nc, ident[:])
 
         stage_words = PASSES * E * H + E * N + T + T
@@ -61,6 +59,7 @@ def tile_moe_wsel_b_relu_p_kernel(
         nc.vector.memset(w1s_all[:].bitcast(I32), 0)
         nc.vector.memset(zeros[:, 0:xs_words], 0)
         nc.vector.tensor_copy(xs[:].rearrange("p s t -> p (s t)").bitcast(I32), zeros[:, 0:xs_words])
+        nc.vector.memset(gate_few[:], 0.0)
         nc.vector.memset(w2s_all[:].bitcast(I32), 0)
 
         w1_at = [4 * E * H * s for s in range(PASSES)]
@@ -106,6 +105,7 @@ def tile_moe_wsel_b_relu_p_kernel(
         load_words(w1_all[0], w1_words[0])
         for q in range(QUADRANTS):
             load_x_scales(q)
+        nc.sync.dma_start(gate_few[0:TILES, :], gate[0, 0, :].rearrange("(j t) -> j t", t=TT))
         load_words(w1_all[1], w1_words[1])
         load_words(x[1], x_words[1])
         for q in range(QUADRANTS):
@@ -187,7 +187,7 @@ def tile_moe_wsel_b_relu_p_kernel(
         gate_sign = keep.tile([P, TILES], F32, name="gate_sign")
 
         def gate_columns():
-            gate_turned = psum.tile([P, P], F32, name="gate_turned", tag="bank6")
+            gate_turned = psum.tile([P, P], F32, name="gate_turned", tag="bank7")
             nc.tensor.transpose(gate_turned[:], gate_few[:], ident[:])
             nc.scalar.activation(gate_size[:], gate_turned[:, 0:TILES], ABS)
             nc.scalar.activation(gate_sign[:], gate_turned[:, 0:TILES], SIGN)

@@ -114,7 +114,7 @@ def tile_moe_wsel_b_relu_p_kernel(
         load_words(w2_all, w2_words[0])
 
         w1s = keep.tile([P, G * H], U8, name="w1s", align_bytes=ALIGN)
-        w1s_dm = keep.tile([P, PACK, P], U8, name="w1s_dm", align_bytes=ALIGN)
+        w1s_dm = stage.tile([P, PACK, P], U8, name="w1s_dm", align_bytes=ALIGN, offset=w1_at[0])
         w1 = [
             [keep.tile([P, H], U32, name="w1_%d_%d" % (s, r), align_bytes=ALIGN) for r in range(G)]
             for s in range(PASSES)
@@ -123,13 +123,13 @@ def tile_moe_wsel_b_relu_p_kernel(
             entries = slice(r * H // PER_COLUMN, (r + 1) * H // PER_COLUMN)
             nc.vector.tensor_copy(w1s[:, r * H : (r + 1) * H], w1s_all[:].indirect(list1[:, entries]))
         warm = psum.tile([P, T], F32, name="warm", tag="bank7")
-        for i in range(4):
+        for planes in [x[0][:].bitcast(U8)] * 2 + [w1s[:]] * 3:
             nc.tensor.matmul_mx(
                 warm[:],
                 lhsT=x[0][:, 0:P].bitcast(FP8X4),
-                lhsT_scale=w1s[:, 0:P],
+                lhsT_scale=planes[:, 0:P],
                 rhs=x[0][:].bitcast(FP8X4),
-                rhs_scale=w1s[:, 0:T],
+                rhs_scale=planes[:, 0:T],
                 start=True,
                 stop=True,
             )
@@ -274,11 +274,11 @@ def tile_moe_wsel_b_relu_p_kernel(
             nc.sync.dma_start(out_hbm[:, :, j * TT : (j + 1) * TT], result[:])
 
         gate_columns()
-        permute_scales()
         gather_w1(0, 0)
         for j in range(TILES):
             first_pass(j, 0, 0)
         gather_w1(0, 1)
+        permute_scales()
         for j in range(TILES - 1):
             first_pass(j, 1, 0)
         for r in range(G):

@@ -100,7 +100,7 @@ def tile_moe_wsel_b_relu_p_kernel(
         nc.sync.dma_start(list1[:], offs)
         load_words(x[0], x_words[0])
         nc.sync.dma_start(list2[:], offs2)
-        for q in range(QUADRANTS):
+        for q in (2, 3, 0, 1):
             load_w1_scales(q)
         load_words(w1_all[0], w1_words[0])
         for q in range(QUADRANTS):

@@ -87,14 +87,14 @@ def tile_moe_wsel_b_relu_p_kernel(
 
         def load_x_scales(q):
             nc.sync.dma_start(
-                xs[:].bitcast(I32)[32 * q : 32 * q + 4],
-                x_scales.bitcast(I32)[:, 4 * q : 4 * q + 4, :].rearrange("s j t -> j s t"),
+                xs[:].bitcast(I32)[q:P:32],
+                x_scales.bitcast(I32)[:, q:16:4, :].rearrange("s j t -> j s t"),
             )
 
         def load_w2_scales(q):
             nc.sync.dma_start(
-                w2s_all[:].bitcast(I32)[32 * q + W2_ROW : 32 * q + W2_ROW + 4, :],
-                w2_scales.bitcast(I32)[0, 4 * q : 4 * q + 4, :],
+                w2s_all[:].bitcast(I32)[W2_ROW + q : P : 32, :],
+                w2_scales.bitcast(I32)[0, q:16:4, :],
             )
 
         nc.sync.dma_start(list1[:], offs)

@@ -142,10 +142,15 @@ def tile_moe_wsel_b_relu_p_kernel(
 
         def gather_w1(s, r):
             entries = slice(r * H // PER_COLUMN, (r + 1) * H // PER_COLUMN)
-            dst = w1[s][r][:].rearrange("p (m d) -> p m d", d=PACK)
-            if r == 1:
-                dst = w1[s][r][:].rearrange("p (d m) -> p m d", d=PACK)
-            nc.vector.tensor_copy(dst, w1_all[s][:].indirect(list1[:, entries]))
+            if r == 0:
+                nc.vector.tensor_copy(w1[s][r][:], w1_all[s][:].indirect(list1[:, entries]))
+            else:
+                listed = keep.tile([P, H], U32, name="w1_listed%d" % s, align_bytes=ALIGN)
+                nc.vector.tensor_copy(listed[:], w1_all[s][:].indirect(list1[:, entries]))
+                nc.vector.tensor_copy(
+                    w1[s][r][:].bitcast(I32).rearrange("p (d a i) -> p a d i", d=PACK, i=PACK),
+                    listed[:].bitcast(I32).rearrange("p (a i d) -> p a d i", d=PACK, i=PACK),
+                )
 
         sums = {}
         sum_bank = {(0, 0): 0, (1, 0): 1, (2, 0): 2, (3, 0): 3, (0, 1): 4, (1, 1): 5, (2, 1): 7, (3, 1): 3}

@@ -97,8 +97,8 @@ def tile_moe_wsel_b_relu_p_kernel(
                 w2_scales.bitcast(I32)[0, q:16:4, :],
             )
 
-        nc.sync.dma_start(list1[:], offs)
         load_words(x[0], x_words[0])
+        nc.sync.dma_start(list1[:], offs)
         nc.sync.dma_start(list2[:], offs2)
         for q in (2, 3, 0, 1):
             load_w1_scales(q)
@@ -249,9 +249,6 @@ def tile_moe_wsel_b_relu_p_kernel(
                 h[j][:].rearrange("p r c -> p (r c)"),
             )
 
-        def quantise_one(j, r):
-            nc.vector.quantize_mx(hq[j][:, r, :].bitcast(FP8X4), hs[j][:, r, :], h[j][:, r, :])
-
         out_hbm = out.rearrange("(c p) t -> p c t", p=P)
 
         def second_pass(dst, c, r, j):
@@ -316,16 +313,14 @@ def tile_moe_wsel_b_relu_p_kernel(
         quantise(1)
         direct(3)
         second_layer(1, False)
-        quantise_one(3, 0)
         quantise(2)
         second_layer(2, False)
+        quantise(3)
         last_sum = [psum.tile([P, TT], F32, name="last_sum%d" % c, tag="bank%d" % (1 + 2 * c)) for c in range(OUT_TILES)]
-        for c in range(OUT_TILES):
-            second_pass(last_sum[c][:], c, 0, 3)
-        quantise_one(3, 1)
         last = [keep.tile([P, TT], F32, name="last%d" % c) for c in range(OUT_TILES)]
         for c in range(OUT_TILES):
-            second_pass(last_sum[c][:], c, 1, 3)
+            for r in range(G):
+                second_pass(last_sum[c][:], c, r, 3)
         nc.vector.tensor_copy(last[0][:], last_sum[0][:])
         nc.sync.dma_start(out_hbm[:, 0, 3 * TT : 4 * TT], last[0][:])
         nc.scalar.copy(last[1][:], last_sum[1][:])

@@ -154,7 +154,7 @@ def tile_moe_wsel_b_relu_p_kernel(
 
         sums = {}
         sum_bank = {(0, 0): 0, (1, 0): 1, (2, 0): 2, (3, 0): 3, (0, 1): 4, (1, 1): 5, (2, 1): 7, (3, 1): 3}
-        back_bank = [0, 1, 2, 6]
+        back_bank = [0, 1, 2, 1]
         out_bank = [4, 5, 0]
 
         def first_pass(j, r, s):
@@ -303,10 +303,11 @@ def tile_moe_wsel_b_relu_p_kernel(
         nc.vector.tensor_copy(w2[:], w2_all[:].indirect(list2[:]))
         turn(0)
         turn(1)
-        turn(3)
         turn(2)
-        for j in (0, 1, 3, 2):
+        for j in range(TILES - 1):
             copy_back(j)
+        turn(3)
+        copy_back(3)
         direct(2)
         quantise(0)
         second_layer(0, False)
@@ -316,7 +317,7 @@ def tile_moe_wsel_b_relu_p_kernel(
         quantise(2)
         second_layer(2, False)
         quantise(3)
-        last_sum = [psum.tile([P, TT], F32, name="last_sum%d" % c, tag="bank%d" % (1 + 2 * c)) for c in range(OUT_TILES)]
+        last_sum = [psum.tile([P, TT], F32, name="last_sum%d" % c, tag="bank%d" % (6 + c)) for c in range(OUT_TILES)]
         last = [keep.tile([P, TT], F32, name="last%d" % c) for c in range(OUT_TILES)]
         for c in range(OUT_TILES):
             for r in range(G):

from contextlib import ExitStack

import concourse.mybir as mybir
from concourse.masks import make_identity

K, T, E, G, H, N = 1024, 512, 4, 2, 512, 256
FLOPS = 2 * G * T * (K * H + H * N)

F32 = mybir.dt.float32
BF16 = mybir.dt.bfloat16
I32 = mybir.dt.int32
U32 = mybir.dt.uint32
U16 = mybir.dt.uint16
U8 = mybir.dt.uint8
FP8X4 = mybir.dt.float8_e4m3fn_x4
MAX = mybir.AluOpType.max
MULT = mybir.AluOpType.mult
ADD = mybir.AluOpType.add
RELU = mybir.ActivationFunctionType.Relu
COPY = mybir.ActivationFunctionType.Copy
ABS = mybir.ActivationFunctionType.Abs
SIGN = mybir.ActivationFunctionType.Sign

P = 128
PACK = 4
PASSES = K // (P * PACK)
QUADRANTS = 4
PER_COLUMN = 16
TT = 128
TILES = T // TT
HALF = T // 2
OUT_TILES = N // P
W1_ROWS = 4
W2_ROW = 8
ALIGN = 64


def tile_moe_wsel_b_relu_p_kernel(
    tc, x_words, x_scales, w1_words, w1_scales, w2_words, w2_scales, gate, offs, offs2, out
):
    nc = tc.nc
    with ExitStack() as ctx:
        keep = ctx.enter_context(tc.tile_pool(name="keep", bufs=1))
        stage = ctx.enter_context(tc.tile_pool(name="stage", bufs=1))
        psum = ctx.enter_context(tc.psum_pool(name="psum", bufs=1))

        list1 = keep.tile([P, G * H // PER_COLUMN], U16, name="list1")
        list2 = keep.tile([P, G * N // PER_COLUMN], U16, name="list2")
        w1s_all = keep.tile([P, E * H], U8, name="w1s_all", align_bytes=ALIGN)
        w2s_all = keep.tile([P, E * N], U8, name="w2s_all", align_bytes=ALIGN)
        xs = keep.tile([P, PASSES, T], U8, name="xs", align_bytes=ALIGN)
        ident = keep.tile([P, P], F32, name="ident")
        gate_few = keep.tile([P, TT], F32, name="gate_few")
        make_identity(nc, ident[:])

        stage_words = PASSES * E * H + E * N + T + T
        xs_words = PASSES * T // 4
        zeros = stage.tile([P, stage_words], I32, name="zeros", offset=0, align_bytes=ALIGN)
        nc.vector.memset(w1s_all[:].bitcast(I32), 0)
        nc.vector.memset(zeros[:, 0:xs_words], 0)
        nc.vector.tensor_copy(xs[:].rearrange("p s t -> p (s t)").bitcast(I32), zeros[:, 0:xs_words])
        nc.vector.memset(gate_few[:], 0.0)
        nc.vector.memset(w2s_all[:].bitcast(I32), 0)

        w1_at = [4 * E * H * s for s in range(PASSES)]
        w2_at = 4 * E * H * PASSES
        x_at = w2_at + 4 * E * N
        gate_rows_at = x_at + 4 * T
        w1_all = [
            stage.tile([P, E * H], U32, name="w1_all%d" % s, align_bytes=ALIGN, offset=w1_at[s]) for s in range(PASSES)
        ]
        w2_all = stage.tile([P, E * N], U32, name="w2_all", align_bytes=ALIGN, offset=w2_at)
        x = [
            keep.tile([P, T], U32, name="x0", align_bytes=ALIGN),
            stage.tile([P, T], U32, name="x1", align_bytes=ALIGN, offset=x_at),
        ]
        gate_rows = stage.tile([P, T], F32, name="gate_rows", align_bytes=ALIGN, offset=gate_rows_at)

        def load_words(dst, src):
            nc.sync.dma_start(dst[:].bitcast(I32), src.rearrange("p m d -> p (m d)").bitcast(I32))

        def load_w1_scales(q):
            nc.sync.dma_start(
                w1s_all[:].bitcast(I32)[32 * q : 32 * q + W1_ROWS * PASSES, :],
                w1_scales.bitcast(I32)[:, 4 * q : 4 * q + 4, :],
            )

        def load_x_scales(q):
            nc.sync.dma_start(
                xs[:].bitcast(I32)[q:P:32],
                x_scales.bitcast(I32)[:, q:16:4, :].rearrange("s j t -> j s t"),
            )

        def load_w2_scales(q):
            nc.sync.dma_start(
                w2s_all[:].bitcast(I32)[W2_ROW + q : P : 32, :],
                w2_scales.bitcast(I32)[0, q:16:4, :],
            )

        load_words(x[0], x_words[0])
        nc.sync.dma_start(list1[:], offs)
        nc.sync.dma_start(list2[:], offs2)
        for q in (2, 3, 0, 1):
            load_w1_scales(q)
        load_words(w1_all[0], w1_words[0])
        for q in range(QUADRANTS):
            load_x_scales(q)
        nc.sync.dma_start(gate_few[0:TILES, :], gate[0, 0, :].rearrange("(j t) -> j t", t=TT))
        load_words(w1_all[1], w1_words[1])
        load_words(x[1], x_words[1])
        for q in range(QUADRANTS):
            load_w2_scales(q)
        nc.sync.dma_start(gate_rows[:], gate[1])
        load_words(w2_all, w2_words[0])

        w1s = keep.tile([P, G * H], U8, name="w1s", align_bytes=ALIGN)
        w1s_dm = stage.tile([P, PACK, P], U8, name="w1s_dm", align_bytes=ALIGN, offset=w1_at[0])
        w1 = [
            [keep.tile([P, H], U32, name="w1_%d_%d" % (s, r), align_bytes=ALIGN) for r in range(G)]
            for s in range(PASSES)
        ]
        for r in range(G):
            entries = slice(r * H // PER_COLUMN, (r + 1) * H // PER_COLUMN)
            nc.vector.tensor_copy(w1s[:, r * H : (r + 1) * H], w1s_all[:].indirect(list1[:, entries]))
        warm = psum.tile([P, T], F32, name="warm", tag="bank7")
        for planes in [x[0][:].bitcast(U8)] * 2 + [w1s[:]] * 3:
            nc.tensor.matmul_mx(
                warm[:],
                lhsT=x[0][:, 0:P].bitcast(FP8X4),
                lhsT_scale=planes[:, 0:P],
                rhs=x[0][:].bitcast(FP8X4),
                rhs_scale=planes[:, 0:T],
                start=True,
                stop=True,
            )

        def permute_scales():
            nc.vector.tensor_copy(
                w1s_dm[:].rearrange("p d (a m) -> p a d m", m=16),
                w1s[:, H : 2 * H].rearrange("p (a m d) -> p a d m", m=16, d=PACK),
            )

        def gather_w1(s, r):
            entries = slice(r * H // PER_COLUMN, (r + 1) * H // PER_COLUMN)
            if r == 0:
                nc.vector.tensor_copy(w1[s][r][:], w1_all[s][:].indirect(list1[:, entries]))
            else:
                listed = keep.tile([P, H], U32, name="w1_listed%d" % s, align_bytes=ALIGN)
                nc.vector.tensor_copy(listed[:], w1_all[s][:].indirect(list1[:, entries]))
                nc.vector.tensor_copy(
                    w1[s][r][:].bitcast(I32).rearrange("p (d a i) -> p a d i", d=PACK, i=PACK),
                    listed[:].bitcast(I32).rearrange("p (a i d) -> p a d i", d=PACK, i=PACK),
                )

        sums = {}
        sum_bank = {(0, 0): 0, (1, 0): 1, (2, 0): 2, (3, 0): 3, (0, 1): 4, (1, 1): 5, (2, 1): 7, (3, 1): 3}
        back_bank = [0, 1, 2, 1]
        out_bank = [4, 5, 0]

        def first_pass(j, r, s):
            tokens = slice(j * TT, (j + 1) * TT)
            words = x[s][:, tokens].bitcast(FP8X4)
            if s == 0:
                sums[j, r] = psum.tile([P, H], F32, name="sums", tag="bank%d" % sum_bank[j, r])
            if r == 0:
                nc.tensor.matmul_mx(
                    sums[j, r][:],
                    lhsT=words,
                    lhsT_scale=xs[:, s, tokens],
                    rhs=w1[s][r][:].bitcast(FP8X4),
                    rhs_scale=w1s[W1_ROWS * s :, 0:H],
                    start=(s == 0),
                    stop=(s == PASSES - 1),
                )
            else:
                for d in range(PACK):
                    nc.tensor.matmul_mx(
                        sums[j, r][:, d * TT : (d + 1) * TT],
                        lhsT=w1[s][r][:, d * P : (d + 1) * P].bitcast(FP8X4),
                        lhsT_scale=w1s_dm[W1_ROWS * s :, d, :],
                        rhs=words,
                        rhs_scale=xs[:, s, tokens],
                        start=(s == 0 and d == 0),
                        stop=(s == PASSES - 1 and d == PACK - 1),
                    )

        def both_passes(j, r):
            for s in range(PASSES):
                first_pass(j, r, s)

        gate_size = keep.tile([P, TILES], F32, name="gate_size")
        gate_sign = keep.tile([P, TILES], F32, name="gate_sign")

        def gate_columns():
            gate_turned = psum.tile([P, P], F32, name="gate_turned", tag="bank7")
            nc.tensor.transpose(gate_turned[:], gate_few[:], ident[:])
            nc.scalar.activation(gate_size[:], gate_turned[:, 0:TILES], ABS)
            nc.scalar.activation(gate_sign[:], gate_turned[:, 0:TILES], SIGN)

        h_turned, backs = {}, {}
        h, hq, hs = {}, {}, {}
        for j in range(TILES):
            h[j] = keep.tile([P, G, TT * PACK], BF16, name="h%d" % j, align_bytes=ALIGN)
            hq[j] = keep.tile([P, G, TT], U32, name="hq%d" % j, align_bytes=ALIGN)
            hs[j] = keep.tile([P, G, TT], U8, name="hs%d" % j, align_bytes=ALIGN)

        def turned(j):
            h_turned[j] = keep.tile([P, H], BF16, name="h_turned%d" % j, align_bytes=ALIGN)
            nc.scalar.activation(
                h_turned[j][:].rearrange("t (u m e) -> t u m e", u=2, e=2),
                sums[j, 0][:].rearrange("t (m u e) -> t u m e", u=2, e=2),
                RELU,
                scale=gate_size[:, j : j + 1],
            )

        def sign(j, engine):
            flat = h_turned[j][:]
            if engine == "vector":
                nc.vector.tensor_scalar(flat, flat, gate_sign[:, j : j + 1], None, MULT)
            elif engine == "scalar":
                nc.scalar.activation(flat, flat, COPY, scale=gate_sign[:, j : j + 1])
            else:
                nc.gpsimd.tensor_scalar(flat, flat, gate_sign[:, j : j + 1], 0.0, MULT, ADD)

        def turn(j):
            backs[j] = psum.tile([P, 2, TT], F32, name="back", tag="bank%d" % back_bank[j])
            for u in range(2):
                nc.tensor.transpose(backs[j][:, u, :], h_turned[j][:].bitcast(F32)[:, u * P : (u + 1) * P], ident[:])

        def copy_back(j):
            nc.scalar.copy(
                h[j][:, 0, :].bitcast(F32).rearrange("p (t u) -> p t u", u=2), backs[j][:].rearrange("p u t -> p t u")
            )

        def direct(j):
            nc.vector.scalar_tensor_tensor(
                h[j][:, 1, :].rearrange("p (t d) -> p t d", d=PACK),
                sums[j, 1][:].rearrange("p (d t) -> p t d", d=PACK),
                0.0,
                gate_rows[:, j * TT : (j + 1) * TT].unsqueeze(2).to_broadcast([P, TT, PACK]),
                MAX,
                MULT,
            )

        def quantise(j):
            nc.vector.quantize_mx(
                hq[j][:].rearrange("p r t -> p (r t)").bitcast(FP8X4),
                hs[j][:].rearrange("p r t -> p (r t)"),
                h[j][:].rearrange("p r c -> p (r c)"),
            )

        out_hbm = out.rearrange("(c p) t -> p c t", p=P)

        def second_pass(dst, c, r, j):
            cols = slice(r * N + c * P, r * N + (c + 1) * P)
            nc.tensor.matmul_mx(
                dst,
                lhsT=w2[:, cols].bitcast(FP8X4),
                lhsT_scale=w2s[W2_ROW:, cols],
                rhs=hq[j][:, r, :].bitcast(FP8X4),
                rhs_scale=hs[j][:, r, :],
                start=(r == 0),
                stop=(r == G - 1),
            )

        def second_layer(j, on_vector):
            out_sum = psum.tile([P, OUT_TILES, TT], F32, name="out_sum", tag="bank%d" % out_bank[j])
            for c in range(OUT_TILES):
                for r in range(G):
                    second_pass(out_sum[:, c, :], c, r, j)
            result = keep.tile([P, OUT_TILES, TT], F32, name="result%d" % j)
            if on_vector:
                nc.vector.tensor_copy(result[:], out_sum[:])
            else:
                nc.scalar.copy(result[:], out_sum[:])
            nc.sync.dma_start(out_hbm[:, :, j * TT : (j + 1) * TT], result[:])

        gate_columns()
        gather_w1(0, 0)
        for j in range(TILES):
            first_pass(j, 0, 0)
        gather_w1(0, 1)
        permute_scales()
        for j in range(TILES - 1):
            first_pass(j, 1, 0)
        for r in range(G):
            gather_w1(1, r)
        w2s = stage.tile([P, G * N], U8, name="w2s", align_bytes=ALIGN, offset=w1_at[1])
        nc.vector.tensor_copy(w2s[:], w2s_all[:].indirect(list2[:]))
        for j in range(TILES):
            first_pass(j, 0, 1)
        for j in range(TILES - 1):
            first_pass(j, 1, 1)
        for j in range(TILES):
            turned(j)
        both_passes(TILES - 1, 1)
        for j in range(3):
            sign(j, "gpsimd")
        sign(3, "scalar")
        direct(0)
        direct(1)
        w2 = keep.tile([P, G * N], U32, name="w2", tag="w1_1_0", align_bytes=ALIGN)
        nc.vector.tensor_copy(w2[:], w2_all[:].indirect(list2[:]))
        turn(0)
        turn(1)
        turn(2)
        for j in range(TILES - 1):
            copy_back(j)
        turn(3)
        copy_back(3)
        direct(2)
        quantise(0)
        second_layer(0, False)
        quantise(1)
        direct(3)
        second_layer(1, False)
        quantise(2)
        second_layer(2, False)
        quantise(3)
        last_sum = [psum.tile([P, TT], F32, name="last_sum%d" % c, tag="bank%d" % (6 + c)) for c in range(OUT_TILES)]
        last = [keep.tile([P, TT], F32, name="last%d" % c) for c in range(OUT_TILES)]
        for c in range(OUT_TILES):
            for r in range(G):
                second_pass(last_sum[c][:], c, r, 3)
        nc.vector.tensor_copy(last[0][:], last_sum[0][:])
        nc.sync.dma_start(out_hbm[:, 0, 3 * TT : 4 * TT], last[0][:])
        nc.scalar.copy(last[1][:], last_sum[1][:])
        nc.scalar.dma_start(out_hbm[:, 1, 3 * TT : 4 * TT], last[1][:])
